import numpy as np
import ml_dtypes


def mxq(x, axis, fmt="e4m3"):
    dtype, down = {"e4m3": (ml_dtypes.float8_e4m3fn, 7), "e5m2": (ml_dtypes.float8_e5m2, 14)}[fmt]
    v = np.moveaxis(np.asarray(x, np.float32).astype(ml_dtypes.bfloat16).astype(np.float64), axis, -1)
    blocks = v.reshape(v.shape[:-1] + (-1, 32))
    amax = np.abs(blocks).max(-1, keepdims=True)
    byte = np.maximum(np.where(amax > 0, np.frexp(amax)[1] - 1 + 127, 0) - down, 1)
    scale = np.exp2(byte - 127.0)
    codes = (blocks / scale).astype(np.float32).astype(dtype).astype(np.float64)
    return np.moveaxis((codes * scale).reshape(v.shape), -1, axis)


WIDE = False


def mx_kscale(k, group=512):
    if not WIDE:
        return np.ones(k)
    levels = np.array([10, -10, 5, -5, 0])
    if group != 512:
        return np.exp2(np.random.permutation(np.resize(levels, k // group))).repeat(group)
    if k % 512:
        return np.exp2(np.random.permutation(np.resize(levels, k // 32))).repeat(32)
    a = np.empty((k // 512, 16))
    for p in range(k // 512):
        a[p, :8] = np.random.permutation(np.resize(levels, 8))
        for g in range(8):
            far = levels[np.abs(levels - a[p, g]) >= 10]
            a[p, g + 8] = far[np.random.randint(len(far))]
    return np.exp2(a.ravel()).repeat(32)


def f64(x):
    return np.asarray(x).astype(np.float64)


K, R, M, N = 512, 256, 512, 1024


def setup_inputs():
    n = np.random.standard_normal
    s = mx_kscale(K)[:, None]
    z = mx_kscale(R, 0)
    return {
        "x": (n((K, N)) * s).astype(np.float32),
        "w": (n((K, M)) / np.sqrt(K) / s).astype(np.float32),
        "a": (n((K, R)) / np.sqrt(K) / s * z).astype(np.float32),
        "bb": (n((R, M)) / np.sqrt(R) / z[:, None]).astype(np.float32),
        "b": (0.5 * n((M, 1))).astype(np.float32),
    }


def reference(x, w, a, bb, b):
    xq = mxq(f64(x), 0, "e4m3")
    z = mxq(f64(a), 0, "e4m3").T @ xq
    y = (mxq(f64(w), 0, "e4m3").T @ xq) + (mxq(f64(bb), 0, "e4m3").T @ mxq(z, 0, "e4m3"))
    y = y + f64(b)
    return y

@@ -1,0 +1,200 @@
+from contextlib import ExitStack
+
+import concourse.mybir as mybir
+
+K, R, M, N = 512, 256, 512, 1024
+FLOPS = 2 * N * (K * M + K * R + R * M)
+
+F32 = mybir.dt.float32
+BF16 = mybir.dt.bfloat16
+U32 = mybir.dt.uint32
+I32 = mybir.dt.int32
+U8 = mybir.dt.uint8
+FP8X4 = mybir.dt.float8_e4m3fn_x4
+ACT = mybir.ActivationFunctionType
+ALU = mybir.AluOpType
+
+P = 128
+H = 64
+W = 256
+NT = 128
+LOADS = ["bb","a","x0","wb","wa","x1","x2","x3"]
+ASG = {"ibb0":"S","ibb1":"S","ia0":"V","ia1":"V","iwa0":"V","iwa1":"S","iwb0":"S","iwb1":"V","ix00":"S","ix01":"V","ix10":"V","ix11":"V","ix20":"S","ix21":"V","ix30":"V","ix31":"V","zc0":"S","mode0a":"W","mode0b":"W","zc1":"S","mode1a":"B","mode1b":"W","zc2":"S","mode2a":"W","mode2b":"W","zc3":"S","mode3a":"W","mode3b":"W"}
+ORDER = ["ia0","ibb0","ibb1","ix00","ia1","qbb","swap","ix01","qa","iwb0","qx0","iwb1","iwa1","zm0","qwb","wm0b","iwa0","zc0","qwa","ix11","ix10","c0b","zq0","wm0a","bm0b","c0a","ix20","qx1","ix21","zm1","d0b","bm0a","qx2","d0a","wm1b","wm2a","zc1","zq1","ix30","ix31","c1b","zm2","bm1b","bm1a","qx3","c2a","zc2","wm2b","c1a","wm1a","zm3","d1b","c2b","zq2","zc3","d1a","bm2a","d2a","wm3a","c3a","bm2b","zq3","wm3b","bm3a","c3b","d2b","bm3b","d3a","d3b"]
+
+
+def tile_rows_lora_bias_kernel(tc, x, w, a, bb, b, out):
+    nc = tc.nc
+    with ExitStack() as ctx:
+        keep = ctx.enter_context(tc.tile_pool(name="keep", bufs=1))
+        psum = ctx.enter_context(tc.psum_pool(name="psum", bufs=1))
+        units = ["bb", "a", "wa", "wb", "x0", "x1", "x2", "x3"]
+        raw = {u: keep.tile([P, 4, W], F32, name="raw_" + u, align_bytes=64) for u in units}
+        grp = {u: keep.tile([P, W * 4], BF16, name="grp_" + u, align_bytes=64) for u in units}
+        plain = ["wa", "wb", "x0", "x1", "x2", "x3"]
+        codes = {u: keep.tile([P, W], U32, name="codes_" + u, align_bytes=256) for u in plain}
+        scales = {u: keep.tile([P, W], U8, name="scales_" + u, align_bytes=256) for u in plain}
+        a_codes = keep.tile([P, 9 * H], U32, name="a_codes", align_bytes=256)
+        a_scales = keep.tile([P, 9 * H], U8, name="a_scales", align_bytes=256)
+        bb_own = keep.tile([P, W + W // 4], U32, name="bb_own", align_bytes=256)
+        bb_other = keep.tile([P, W + W // 4], U32, name="bb_other", align_bytes=256)
+        z_grp = [keep.tile([P, NT * 4], BF16, name="z_grp%d" % c, align_bytes=64) for c in range(4)]
+        z_codes = [keep.tile([P, NT], U32, name="z_codes%d" % c, align_bytes=256) for c in range(4)]
+        z_scales = [keep.tile([P, NT], U8, name="z_scales%d" % c, align_bytes=256) for c in range(4)]
+        y = {(c, m): keep.tile([P, 2, W], F32, name="y%d%s" % (c, m), align_bytes=64) for c in range(4) for m in "ab"}
+        bias = keep.tile([P, 4], F32, name="bias")
+        warm_in = keep.tile([P, 1], F32, name="warm_in")
+        warm_out = keep.tile([P, 1], F32, name="warm_out")
+        z_bank = [psum.tile([P, 4, NT], F32, name="z_bank%d" % i) for i in range(2)]
+        w_bank = [psum.tile([P, 2, W], F32, name="w_bank%d" % i) for i in range(2)]
+        r_bank = {(h, m): psum.tile([P, 4, NT], F32, name="r_bank%d%s" % (h, m)) for h in range(2) for m in "ab"}
+        w_bank_of = {}
+
+        ctx.enter_context(tc.manual_schedule())
+
+        def load(u):
+            if u == "bb":
+                rows = bb.rearrange("(p j) m -> p j m", j=4)
+                nc.sync.dma_start(out=raw[u][0:H], in_=rows[:, :, 0:W])
+                nc.scalar.dma_start(out=raw[u][H:P], in_=rows[:, :, W:M])
+                return
+            if u == "a":
+                src = a.rearrange("(p j) r -> p j r", j=4)
+            elif u[0] == "w":
+                m0 = W * "ab".index(u[1])
+                src = w.rearrange("(p j) m -> p j m", j=4)[:, :, m0:m0 + W]
+            else:
+                n0 = W * int(u[1])
+                src = x.rearrange("(p j) n -> p j n", j=4)[:, :, n0:n0 + W]
+            nc.sync.dma_start(out=raw[u][:], in_=src)
+
+        def copy_on(e, dst, src):
+            if e == "V":
+                nc.vector.tensor_copy(out=dst, in_=src)
+            elif e == "S":
+                nc.scalar.copy(out=dst, in_=src)
+            else:
+                nc.gpsimd.tensor_scalar(out=dst, in0=src, scalar1=1.0, scalar2=0.0, op0=ALU.mult, op1=ALU.add)
+
+        def interleave(u, half):
+            e = ASG["i%s%d" % (u, half)]
+            if u == "a":
+                q = slice(32 * half, 32 * half + 32)
+                dst = grp[u][:].rearrange("p (s q j) -> p q s j", s=4, j=4)[:, q]
+                src = raw[u][:].rearrange("p j (q s) -> p q s j", s=4)[:, q]
+            else:
+                c = slice(32 * half, 32 * half + 32)
+                dst = grp[u][:].rearrange("p (c i j) -> p c j i", i=4, j=4)[:, c]
+                src = raw[u][:].rearrange("p j (c i) -> p c j i", i=4)[:, c]
+            copy_on(e, dst, src)
+
+        def quantize(u):
+            if u == "a":
+                for s in range(4):
+                    cols = slice(H + P * s, P + P * s)
+                    nc.vector.quantize_mx(out=a_codes[:, cols].bitcast(FP8X4), scales=a_scales[:, cols],
+                                          in_=grp[u][:, W * s:W * (s + 1)])
+            elif u == "bb":
+                nc.vector.quantize_mx(out=bb_own[:, 0:W].bitcast(FP8X4), scales=bb_own[:, W:W + W // 4].bitcast(U8),
+                                      in_=grp[u][:])
+            else:
+                nc.vector.quantize_mx(out=codes[u][:].bitcast(FP8X4), scales=scales[u][:], in_=grp[u][:])
+
+        def swap():
+            nc.scalar.dma_start(out=bb_other[0:H, :].bitcast(I32), in_=bb_own[H:P, :].bitcast(I32))
+            nc.scalar.dma_start(out=bb_other[H:P, :].bitcast(I32), in_=bb_own[0:H, :].bitcast(I32))
+
+        def z_matmul(c):
+            u = "x%d" % c
+            for s in range(4):
+                for h in range(2):
+                    win = slice(P * s + H * (1 - h), P * s + H * (1 - h) + P)
+                    cols = slice(NT * h, NT * (h + 1))
+                    nc.tensor.matmul_mx(out=z_bank[c % 2][:, s, :], lhsT=a_codes[:, win].bitcast(FP8X4),
+                                        lhsT_scale=a_scales[:, win], rhs=codes[u][:, cols].bitcast(FP8X4),
+                                        rhs_scale=scales[u][:, cols], start=(h == 0), stop=(h == 1))
+
+        def z_copy(c):
+            copy_on(ASG["zc%d" % c], z_grp[c][:].rearrange("p (n s) -> p n s", s=4),
+                    z_bank[c % 2][:].rearrange("p s n -> p n s"))
+
+        def z_quantize(c):
+            nc.vector.quantize_mx(out=z_codes[c][:].bitcast(FP8X4), scales=z_scales[c][:], in_=z_grp[c][:])
+
+        def w_matmul(c, m):
+            bank = w_bank[len(w_bank_of) % 2]
+            w_bank_of[(c, m)] = bank
+            u, wu = "x%d" % c, "w" + m
+            for t in range(2):
+                mc = slice(P * t, P * (t + 1))
+                for h in range(2):
+                    cols = slice(NT * h, NT * (h + 1))
+                    nc.tensor.matmul_mx(out=bank[:, t, cols], lhsT=codes[wu][:, mc].bitcast(FP8X4),
+                                        lhsT_scale=scales[wu][:, mc], rhs=codes[u][:, cols].bitcast(FP8X4),
+                                        rhs_scale=scales[u][:, cols], start=True, stop=True)
+
+        def b_matmul(c, m):
+            for t in range(2):
+                for h in range(2):
+                    rows = slice(H * h, H * (h + 1))
+                    src = bb_own if "ab".index(m) == h else bb_other
+                    nc.tensor.matmul_mx(out=r_bank[(h, m)][:, t, :], lhsT=src[rows, P * t:P * (t + 1)].bitcast(FP8X4),
+                                        lhsT_scale=src[rows, W + 32 * t:W + 32 * (t + 1)].bitcast(U8),
+                                        rhs=z_codes[c][rows, :].bitcast(FP8X4), rhs_scale=z_scales[c][rows, :],
+                                        start=True, stop=True)
+
+        def first_sum(c, m):
+            yt = y[(c, m)]
+            if ASG["mode%d%s" % (c, m)] == "W":
+                for t in range(2):
+                    mt = 2 * "ab".index(m) + t
+                    nc.scalar.activation(out=yt[:, t, :], in_=w_bank_of[(c, m)][:, t, :], func=ACT.Identity,
+                                         bias=bias[:, mt:mt + 1])
+            else:
+                for h in range(2):
+                    nc.scalar.copy(out=yt[:, :, NT * h:NT * (h + 1)], in_=r_bank[(h, m)][:, 0:2, :])
+
+        def second_sum(c, m):
+            yt = y[(c, m)]
+            if ASG["mode%d%s" % (c, m)] == "W":
+                for h in range(2):
+                    part = yt[:, :, NT * h:NT * (h + 1)]
+                    nc.vector.tensor_tensor(out=part, in0=r_bank[(h, m)][:, 0:2, :], in1=part, op=ALU.add)
+            else:
+                for t in range(2):
+                    mt = 2 * "ab".index(m) + t
+                    nc.vector.scalar_tensor_tensor(out=yt[:, t, :], in0=w_bank_of[(c, m)][:, t, :],
+                                                   scalar=bias[:, mt:mt + 1], in1=yt[:, t, :], op0=ALU.add, op1=ALU.add)
+            t0 = 2 * "ab".index(m)
+            nc.sync.dma_start(out=out.rearrange("(t p) n -> p t n", p=P)[:, t0:t0 + 2, W * c:W * (c + 1)], in_=yt[:])
+
+        for u in LOADS:
+            load(u)
+        with nc.allow_non_contiguous_dma(reason="one bias value to a partition"):
+            nc.scalar.dma_start(out=bias[:], in_=b.rearrange("(t p) o -> p (t o)", p=P))
+        nc.vector.memset(warm_in[:], 0.0)
+        nc.scalar.activation(out=warm_out[:], in_=warm_in[:], func=ACT.Identity)
+        nc.vector.memset(bb_own[:, W:W + W // 4], 0)
+        nc.vector.memset(a_codes[:], 0)
+        nc.vector.memset(a_scales[:].bitcast(U32), 0)
+        for task in ORDER:
+            if task == "swap":
+                swap()
+            elif task[0] == "i":
+                interleave(task[1:-1], int(task[-1]))
+            elif task[0] == "q":
+                quantize(task[1:])
+            elif task[:2] == "zm":
+                z_matmul(int(task[2]))
+            elif task[:2] == "zc":
+                z_copy(int(task[2]))
+            elif task[:2] == "zq":
+                z_quantize(int(task[2]))
+            elif task[:2] == "wm":
+                w_matmul(int(task[2]), task[3])
+            elif task[:2] == "bm":
+                b_matmul(int(task[2]), task[3])
+            elif task[0] == "c":
+                first_sum(int(task[1]), task[2])
+            else:
+                second_sum(int(task[1]), task[2])

@@ -11,16 +11,21 @@ U32 = mybir.dt.uint32
 I32 = mybir.dt.int32
 U8 = mybir.dt.uint8
 FP8X4 = mybir.dt.float8_e4m3fn_x4
-ACT = mybir.ActivationFunctionType
-ALU = mybir.AluOpType
+ADD = mybir.AluOpType.add
+IDENTITY = mybir.ActivationFunctionType.Identity
 
 P = 128
-H = 64
-W = 256
-NT = 128
-LOADS = ["bb","a","x0","wb","wa","x1","x2","x3"]
-ASG = {"ibb0":"S","ibb1":"S","ia0":"V","ia1":"V","iwa0":"V","iwa1":"S","iwb0":"S","iwb1":"V","ix00":"S","ix01":"V","ix10":"V","ix11":"V","ix20":"S","ix21":"V","ix30":"V","ix31":"V","zc0":"S","mode0a":"W","mode0b":"W","zc1":"S","mode1a":"B","mode1b":"W","zc2":"S","mode2a":"W","mode2b":"W","zc3":"S","mode3a":"W","mode3b":"W"}
-ORDER = ["ia0","ibb0","ibb1","ix00","ia1","qbb","swap","ix01","qa","iwb0","qx0","iwb1","iwa1","zm0","qwb","wm0b","iwa0","zc0","qwa","ix11","ix10","c0b","zq0","wm0a","bm0b","c0a","ix20","qx1","ix21","zm1","d0b","bm0a","qx2","d0a","wm1b","wm2a","zc1","zq1","ix30","ix31","c1b","zm2","bm1b","bm1a","qx3","c2a","zc2","wm2b","c1a","wm1a","zm3","d1b","c2b","zq2","zc3","d1a","bm2a","d2a","wm3a","c3a","bm2b","zq3","wm3b","bm3a","c3b","d2b","bm3b","d3a","d3b"]
+ROWS = 64
+PACK = 4
+GROUP = 256
+COLS = 128
+SCALE_WORDS = GROUP // 4
+QUAD = 32
+WHOLE_BANKS = 4
+ROW_SETS = 2
+
+VECTOR, SCALAR = "vector", "scalar"
+LEFT, RIGHT, WHOLE = slice(0, GROUP // 2), slice(GROUP // 2, GROUP), slice(0, GROUP)
 
 
 def tile_rows_lora_bias_kernel(tc, x, w, a, bb, b, out):
@@ -28,173 +33,247 @@ def tile_rows_lora_bias_kernel(tc, x, w, a, bb, b, out):
     with ExitStack() as ctx:
         keep = ctx.enter_context(tc.tile_pool(name="keep", bufs=1))
         psum = ctx.enter_context(tc.psum_pool(name="psum", bufs=1))
-        units = ["bb", "a", "wa", "wb", "x0", "x1", "x2", "x3"]
-        raw = {u: keep.tile([P, 4, W], F32, name="raw_" + u, align_bytes=64) for u in units}
-        grp = {u: keep.tile([P, W * 4], BF16, name="grp_" + u, align_bytes=64) for u in units}
-        plain = ["wa", "wb", "x0", "x1", "x2", "x3"]
-        codes = {u: keep.tile([P, W], U32, name="codes_" + u, align_bytes=256) for u in plain}
-        scales = {u: keep.tile([P, W], U8, name="scales_" + u, align_bytes=256) for u in plain}
-        a_codes = keep.tile([P, 9 * H], U32, name="a_codes", align_bytes=256)
-        a_scales = keep.tile([P, 9 * H], U8, name="a_scales", align_bytes=256)
-        bb_own = keep.tile([P, W + W // 4], U32, name="bb_own", align_bytes=256)
-        bb_other = keep.tile([P, W + W // 4], U32, name="bb_other", align_bytes=256)
-        z_grp = [keep.tile([P, NT * 4], BF16, name="z_grp%d" % c, align_bytes=64) for c in range(4)]
-        z_codes = [keep.tile([P, NT], U32, name="z_codes%d" % c, align_bytes=256) for c in range(4)]
-        z_scales = [keep.tile([P, NT], U8, name="z_scales%d" % c, align_bytes=256) for c in range(4)]
-        y = {(c, m): keep.tile([P, 2, W], F32, name="y%d%s" % (c, m), align_bytes=64) for c in range(4) for m in "ab"}
-        bias = keep.tile([P, 4], F32, name="bias")
-        warm_in = keep.tile([P, 1], F32, name="warm_in")
-        warm_out = keep.tile([P, 1], F32, name="warm_out")
-        z_bank = [psum.tile([P, 4, NT], F32, name="z_bank%d" % i) for i in range(2)]
-        w_bank = [psum.tile([P, 2, W], F32, name="w_bank%d" % i) for i in range(2)]
-        r_bank = {(h, m): psum.tile([P, 4, NT], F32, name="r_bank%d%s" % (h, m)) for h in range(2) for m in "ab"}
-        w_bank_of = {}
 
-        ctx.enter_context(tc.manual_schedule())
+        raw_tiles = {name: keep.tile([P, PACK, GROUP], F32, name="raw_" + name, align_bytes=64)
+                     for name in ("bb", "a", "w0", "w1")}
+        raw_x = [keep.tile([P, PACK, 2 * GROUP], F32, name="raw_x%d" % pair, align_bytes=64) for pair in range(2)]
+        raw = {name: tile[:] for name, tile in raw_tiles.items()}
+        for c in range(4):
+            raw["x%d" % c] = raw_x[c // 2][:, :, GROUP * (c % 2):GROUP * (c % 2 + 1)]
+        grouped = {name: keep.tile([P, GROUP * PACK], BF16, name="grouped_" + name, align_bytes=64) for name in raw}
+        plain = ("w0", "w1", "x0", "x1", "x2", "x3")
+        codes = {name: keep.tile([P, GROUP], U32, name="codes_" + name, align_bytes=256) for name in plain}
+        scales = {name: keep.tile([P, GROUP], U8, name="scales_" + name, align_bytes=256) for name in plain}
+        a_codes = keep.tile([P, 9 * ROWS], U32, name="a_codes", align_bytes=256)
+        a_scales = keep.tile([P, 9 * ROWS], U8, name="a_scales", align_bytes=256)
+        bb_own = keep.tile([P, GROUP + SCALE_WORDS], U32, name="bb_own", align_bytes=256)
+        bb_other = keep.tile([P, GROUP + SCALE_WORDS], U32, name="bb_other", align_bytes=256)
+        z_grouped = [keep.tile([P, COLS * PACK], BF16, name="z_grouped%d" % c, align_bytes=64) for c in range(4)]
+        z_codes = [keep.tile([P, COLS], U32, name="z_codes%d" % c, align_bytes=256) for c in range(4)]
+        z_scales = [keep.tile([P, COLS], U8, name="z_scales%d" % c, align_bytes=256) for c in range(4)]
+        y = {(pair, t): keep.tile([P, 2 * GROUP], F32, name="y%d%d" % (pair, t), align_bytes=64)
+             for pair in range(2) for t in range(4)}
+        bias = keep.tile([P, QUAD], F32, name="bias", align_bytes=64)
+        bias_rows = keep.tile([P, QUAD], F32, name="bias_rows", align_bytes=64)
+        table_in = keep.tile([P, 1], F32, name="table_in")
+        table_out = keep.tile([P, 1], F32, name="table_out")
 
-        def load(u):
-            if u == "bb":
-                rows = bb.rearrange("(p j) m -> p j m", j=4)
-                nc.sync.dma_start(out=raw[u][0:H], in_=rows[:, :, 0:W])
-                nc.scalar.dma_start(out=raw[u][H:P], in_=rows[:, :, W:M])
-                return
-            if u == "a":
-                src = a.rearrange("(p j) r -> p j r", j=4)
-            elif u[0] == "w":
-                m0 = W * "ab".index(u[1])
-                src = w.rearrange("(p j) m -> p j m", j=4)[:, :, m0:m0 + W]
+        whole_banks = [psum.tile([P, PACK * COLS], F32, name="whole_bank%d" % i) for i in range(WHOLE_BANKS)]
+        row_banks = [[psum.tile([P, PACK, COLS], F32, name="row_bank%d%d" % (half, i)) for half in range(2)]
+                     for i in range(ROW_SETS)]
+        whole_bank_of = {}
+        row_banks_of = {}
+
+        def by_half(tile_columns):
+            return tile_columns.rearrange("p (c half n) -> p half c n", c=2, half=2)
+
+        def interleave(engine, name, cols):
+            dst = grouped[name][:].rearrange("p (c j) -> p c j", j=PACK)[:, cols]
+            src = raw[name].rearrange("p j c -> p c j")[:, cols]
+            if engine == VECTOR:
+                nc.vector.tensor_copy(out=dst.rearrange("p (c i) j -> p c j i", i=4),
+                                      in_=src.rearrange("p (c i) j -> p c j i", i=4))
             else:
-                n0 = W * int(u[1])
-                src = x.rearrange("(p j) n -> p j n", j=4)[:, :, n0:n0 + W]
-            nc.sync.dma_start(out=raw[u][:], in_=src)
-
-        def copy_on(e, dst, src):
-            if e == "V":
-                nc.vector.tensor_copy(out=dst, in_=src)
-            elif e == "S":
                 nc.scalar.copy(out=dst, in_=src)
-            else:
-                nc.gpsimd.tensor_scalar(out=dst, in0=src, scalar1=1.0, scalar2=0.0, op0=ALU.mult, op1=ALU.add)
 
-        def interleave(u, half):
-            e = ASG["i%s%d" % (u, half)]
-            if u == "a":
-                q = slice(32 * half, 32 * half + 32)
-                dst = grp[u][:].rearrange("p (s q j) -> p q s j", s=4, j=4)[:, q]
-                src = raw[u][:].rearrange("p j (q s) -> p q s j", s=4)[:, q]
-            else:
-                c = slice(32 * half, 32 * half + 32)
-                dst = grp[u][:].rearrange("p (c i j) -> p c j i", i=4, j=4)[:, c]
-                src = raw[u][:].rearrange("p j (c i) -> p c j i", i=4)[:, c]
-            copy_on(e, dst, src)
+        def interleave_a():
+            nc.vector.tensor_copy(out=grouped["a"][:].rearrange("p (s q j) -> p q s j", s=PACK, j=PACK),
+                                  in_=raw["a"].rearrange("p j (q s) -> p q s j", s=PACK))
 
-        def quantize(u):
-            if u == "a":
-                for s in range(4):
-                    cols = slice(H + P * s, P + P * s)
-                    nc.vector.quantize_mx(out=a_codes[:, cols].bitcast(FP8X4), scales=a_scales[:, cols],
-                                          in_=grp[u][:, W * s:W * (s + 1)])
-            elif u == "bb":
-                nc.vector.quantize_mx(out=bb_own[:, 0:W].bitcast(FP8X4), scales=bb_own[:, W:W + W // 4].bitcast(U8),
-                                      in_=grp[u][:])
-            else:
-                nc.vector.quantize_mx(out=codes[u][:].bitcast(FP8X4), scales=scales[u][:], in_=grp[u][:])
+        def quantize(name):
+            nc.vector.quantize_mx(out=codes[name][:].bitcast(FP8X4), scales=scales[name][:], in_=grouped[name][:])
 
-        def swap():
-            nc.scalar.dma_start(out=bb_other[0:H, :].bitcast(I32), in_=bb_own[H:P, :].bitcast(I32))
-            nc.scalar.dma_start(out=bb_other[H:P, :].bitcast(I32), in_=bb_own[0:H, :].bitcast(I32))
+        def quantize_a():
+            for s in range(PACK):
+                strip = slice(ROWS * (2 * s + 1), ROWS * (2 * s + 2))
+                nc.vector.quantize_mx(out=a_codes[:, strip].bitcast(FP8X4), scales=a_scales[:, strip],
+                                      in_=grouped["a"][:, ROWS * PACK * s:ROWS * PACK * (s + 1)])
+
+        def quantize_bb():
+            nc.vector.quantize_mx(out=bb_own[:, 0:GROUP].bitcast(FP8X4), scales=bb_own[:, GROUP:].bitcast(U8),
+                                  in_=grouped["bb"][:])
+
+        def exchange_bb_halves():
+            nc.scalar.dma_start(out=bb_other[0:ROWS, :].bitcast(I32), in_=bb_own[ROWS:P, :].bitcast(I32))
+            nc.scalar.dma_start(out=bb_other[ROWS:P, :].bitcast(I32), in_=bb_own[0:ROWS, :].bitcast(I32))
+
+        def transpose_bias():
+            nc.vector.transpose(out=bias[:], in_=bias_rows[:])
+
+        def warm_up():
+            bank = whole_banks[len(whole_bank_of) % WHOLE_BANKS]
+            for s in range(PACK):
+                nc.tensor.matmul_mx(out=bank[:, COLS * s:COLS * (s + 1)], lhsT=a_codes[:, 0:P].bitcast(FP8X4),
+                                    lhsT_scale=a_scales[:, 0:P], rhs=a_codes[:, 0:COLS].bitcast(FP8X4),
+                                    rhs_scale=a_scales[:, 0:COLS], start=True, stop=True)
 
         def z_matmul(c):
-            u = "x%d" % c
-            for s in range(4):
-                for h in range(2):
-                    win = slice(P * s + H * (1 - h), P * s + H * (1 - h) + P)
-                    cols = slice(NT * h, NT * (h + 1))
-                    nc.tensor.matmul_mx(out=z_bank[c % 2][:, s, :], lhsT=a_codes[:, win].bitcast(FP8X4),
-                                        lhsT_scale=a_scales[:, win], rhs=codes[u][:, cols].bitcast(FP8X4),
-                                        rhs_scale=scales[u][:, cols], start=(h == 0), stop=(h == 1))
+            name = "x%d" % c
+            bank = whole_banks[len(whole_bank_of) % WHOLE_BANKS][:].rearrange("p (s n) -> p s n", s=PACK)
+            whole_bank_of[c] = bank
+            for s in range(PACK):
+                for half in range(2):
+                    first = ROWS * (2 * s + 1 - half)
+                    window = slice(first, first + P)
+                    cols = slice(COLS * half, COLS * (half + 1))
+                    nc.tensor.matmul_mx(out=bank[:, s, :], lhsT=a_codes[:, window].bitcast(FP8X4),
+                                        lhsT_scale=a_scales[:, window], rhs=codes[name][:, cols].bitcast(FP8X4),
+                                        rhs_scale=scales[name][:, cols], start=(half == 0), stop=(half == 1))
 
-        def z_copy(c):
-            copy_on(ASG["zc%d" % c], z_grp[c][:].rearrange("p (n s) -> p n s", s=4),
-                    z_bank[c % 2][:].rearrange("p s n -> p n s"))
+        def z_copy(engine, c):
+            dst = z_grouped[c][:].rearrange("p (n s) -> p n s", s=PACK)
+            src = whole_bank_of[c].rearrange("p s n -> p n s")
+            if engine == VECTOR:
+                nc.vector.tensor_copy(out=dst, in_=src)
+            else:
+                nc.scalar.copy(out=dst, in_=src)
 
         def z_quantize(c):
-            nc.vector.quantize_mx(out=z_codes[c][:].bitcast(FP8X4), scales=z_scales[c][:], in_=z_grp[c][:])
+            nc.vector.quantize_mx(out=z_codes[c][:].bitcast(FP8X4), scales=z_scales[c][:], in_=z_grouped[c][:])
 
-        def w_matmul(c, m):
-            bank = w_bank[len(w_bank_of) % 2]
-            w_bank_of[(c, m)] = bank
-            u, wu = "x%d" % c, "w" + m
-            for t in range(2):
-                mc = slice(P * t, P * (t + 1))
-                for h in range(2):
-                    cols = slice(NT * h, NT * (h + 1))
-                    nc.tensor.matmul_mx(out=bank[:, t, cols], lhsT=codes[wu][:, mc].bitcast(FP8X4),
-                                        lhsT_scale=scales[wu][:, mc], rhs=codes[u][:, cols].bitcast(FP8X4),
-                                        rhs_scale=scales[u][:, cols], start=True, stop=True)
+        def w_matmul(pair, t):
+            bank = whole_banks[len(whole_bank_of) % WHOLE_BANKS]
+            whole_bank_of[(pair, t)] = bank
+            w_name = "w%d" % (t // 2)
+            m_cols = slice(P * (t % 2), P * (t % 2 + 1))
+            for i in range(2 * GROUP // COLS):
+                x_name = "x%d" % (2 * pair + i // 2)
+                cols = slice(COLS * (i % 2), COLS * (i % 2 + 1))
+                nc.tensor.matmul_mx(out=bank[:, COLS * i:COLS * (i + 1)], lhsT=codes[w_name][:, m_cols].bitcast(FP8X4),
+                                    lhsT_scale=scales[w_name][:, m_cols], rhs=codes[x_name][:, cols].bitcast(FP8X4),
+                                    rhs_scale=scales[x_name][:, cols], start=True, stop=True)
 
-        def b_matmul(c, m):
-            for t in range(2):
-                for h in range(2):
-                    rows = slice(H * h, H * (h + 1))
-                    src = bb_own if "ab".index(m) == h else bb_other
-                    nc.tensor.matmul_mx(out=r_bank[(h, m)][:, t, :], lhsT=src[rows, P * t:P * (t + 1)].bitcast(FP8X4),
-                                        lhsT_scale=src[rows, W + 32 * t:W + 32 * (t + 1)].bitcast(U8),
+        def bb_matmul(pair, t):
+            banks = row_banks[len(row_banks_of) % ROW_SETS]
+            row_banks_of[(pair, t)] = banks
+            m_cols = slice(P * (t % 2), P * (t % 2 + 1))
+            m_scale_words = slice(GROUP + P // 4 * (t % 2), GROUP + P // 4 * (t % 2 + 1))
+            for i in range(2):
+                c = 2 * pair + i
+                for half in range(2):
+                    rows = slice(ROWS * half, ROWS * (half + 1))
+                    bb_tile = bb_own if t // 2 == half else bb_other
+                    nc.tensor.matmul_mx(out=banks[half][:, i, :], lhsT=bb_tile[rows, m_cols].bitcast(FP8X4),
+                                        lhsT_scale=bb_tile[rows, m_scale_words].bitcast(U8),
                                         rhs=z_codes[c][rows, :].bitcast(FP8X4), rhs_scale=z_scales[c][rows, :],
                                         start=True, stop=True)
 
-        def first_sum(c, m):
-            yt = y[(c, m)]
-            if ASG["mode%d%s" % (c, m)] == "W":
-                for t in range(2):
-                    mt = 2 * "ab".index(m) + t
-                    nc.scalar.activation(out=yt[:, t, :], in_=w_bank_of[(c, m)][:, t, :], func=ACT.Identity,
-                                         bias=bias[:, mt:mt + 1])
-            else:
-                for h in range(2):
-                    nc.scalar.copy(out=yt[:, :, NT * h:NT * (h + 1)], in_=r_bank[(h, m)][:, 0:2, :])
+        def out_tile(pair, t):
+            return out[P * t:P * (t + 1), 2 * GROUP * pair:2 * GROUP * (pair + 1)]
 
-        def second_sum(c, m):
-            yt = y[(c, m)]
-            if ASG["mode%d%s" % (c, m)] == "W":
-                for h in range(2):
-                    part = yt[:, :, NT * h:NT * (h + 1)]
-                    nc.vector.tensor_tensor(out=part, in0=r_bank[(h, m)][:, 0:2, :], in1=part, op=ALU.add)
-            else:
-                for t in range(2):
-                    mt = 2 * "ab".index(m) + t
-                    nc.vector.scalar_tensor_tensor(out=yt[:, t, :], in0=w_bank_of[(c, m)][:, t, :],
-                                                   scalar=bias[:, mt:mt + 1], in1=yt[:, t, :], op0=ALU.add, op1=ALU.add)
-            t0 = 2 * "ab".index(m)
-            nc.sync.dma_start(out=out.rearrange("(t p) n -> p t n", p=P)[:, t0:t0 + 2, W * c:W * (c + 1)], in_=yt[:])
+        def copy_w_sum(pair, t):
+            nc.scalar.activation(out=y[(pair, t)][:], in_=whole_bank_of[(pair, t)][:], func=IDENTITY,
+                                 bias=bias[:, t:t + 1])
 
-        for u in LOADS:
-            load(u)
-        with nc.allow_non_contiguous_dma(reason="one bias value to a partition"):
-            nc.scalar.dma_start(out=bias[:], in_=b.rearrange("(t p) o -> p (t o)", p=P))
-        nc.vector.memset(warm_in[:], 0.0)
-        nc.scalar.activation(out=warm_out[:], in_=warm_in[:], func=ACT.Identity)
-        nc.vector.memset(bb_own[:, W:W + W // 4], 0)
+        def add_bb_sum(pair, t, store_halves=False):
+            for half in range(2):
+                part = by_half(y[(pair, t)][:])[:, half]
+                nc.vector.tensor_tensor(out=part, in0=row_banks_of[(pair, t)][half][:, 0:2, :], in1=part, op=ADD)
+                if store_halves:
+                    nc.sync.dma_start(out=by_half(out_tile(pair, t))[:, half], in_=part)
+            if not store_halves:
+                nc.sync.dma_start(out=out_tile(pair, t), in_=y[(pair, t)][:])
+
+        def copy_bb_sum(pair, t):
+            for half in range(2):
+                nc.scalar.copy(out=by_half(y[(pair, t)][:])[:, half], in_=row_banks_of[(pair, t)][half][:, 0:2, :])
+
+        def add_w_sum(pair, t):
+            nc.vector.scalar_tensor_tensor(out=y[(pair, t)][:], in0=whole_bank_of[(pair, t)][:],
+                                           scalar=bias[:, t:t + 1], in1=y[(pair, t)][:], op0=ADD, op1=ADD)
+            nc.sync.dma_start(out=out_tile(pair, t), in_=y[(pair, t)][:])
+
+        ctx.enter_context(tc.manual_schedule())
+
+        bb_rows = bb.rearrange("(p j) m -> p j m", j=PACK)
+        x_rows = x.rearrange("(p j) n -> p j n", j=PACK)
+        w_rows = w.rearrange("(p j) m -> p j m", j=PACK)
+        nc.sync.dma_start(out=raw_tiles["bb"][0:ROWS], in_=bb_rows[:, :, 0:GROUP])
+        nc.scalar.dma_start(out=raw_tiles["bb"][ROWS:P], in_=bb_rows[:, :, GROUP:M])
+        nc.sync.dma_start(out=raw["a"], in_=a.rearrange("(p j) r -> p j r", j=PACK))
+        nc.sync.dma_start(out=raw_x[0][:], in_=x_rows[:, :, 0:N // 2])
+        nc.sync.dma_start(out=raw_x[1][:], in_=x_rows[:, :, N // 2:N])
+        nc.sync.dma_start(out=raw["w0"], in_=w_rows[:, :, 0:GROUP])
+        nc.sync.dma_start(out=raw["w1"], in_=w_rows[:, :, GROUP:M])
+
+        nc.vector.memset(table_in[:], 0.0)
+        nc.scalar.activation(out=table_out[:], in_=table_in[:], func=IDENTITY)
+
+        nc.gpsimd.memset(bias_rows[:], 0.0)
+        b_rows = b.rearrange("(t q j) o -> q t (j o)", t=4, q=P // QUAD)
+        for q in range(P // QUAD):
+            nc.gpsimd.dma_start(out=bias_rows[QUAD * q:QUAD * q + 4, :], in_=b_rows[q])
+
+        nc.vector.memset(bb_own[:, GROUP:], 0)
         nc.vector.memset(a_codes[:], 0)
         nc.vector.memset(a_scales[:].bitcast(U32), 0)
-        for task in ORDER:
-            if task == "swap":
-                swap()
-            elif task[0] == "i":
-                interleave(task[1:-1], int(task[-1]))
-            elif task[0] == "q":
-                quantize(task[1:])
-            elif task[:2] == "zm":
-                z_matmul(int(task[2]))
-            elif task[:2] == "zc":
-                z_copy(int(task[2]))
-            elif task[:2] == "zq":
-                z_quantize(int(task[2]))
-            elif task[:2] == "wm":
-                w_matmul(int(task[2]), task[3])
-            elif task[:2] == "bm":
-                b_matmul(int(task[2]), task[3])
-            elif task[0] == "c":
-                first_sum(int(task[1]), task[2])
-            else:
-                second_sum(int(task[1]), task[2])
+
+        interleave(VECTOR, "bb", LEFT)
+        interleave(SCALAR, "bb", RIGHT)
+        interleave_a()
+        quantize_a()
+        warm_up()
+        interleave(VECTOR, "x0", WHOLE)
+        interleave(VECTOR, "x1", LEFT)
+        quantize("x0")
+        quantize_bb()
+        interleave(SCALAR, "x1", RIGHT)
+        warm_up()
+        warm_up()
+        z_matmul(0)
+        quantize("x1")
+        exchange_bb_halves()
+        z_matmul(1)
+        z_copy(SCALAR, 0)
+        z_copy(SCALAR, 1)
+        interleave(VECTOR, "x3", WHOLE)
+        interleave(VECTOR, "x2", LEFT)
+        quantize("x3")
+        z_matmul(3)
+        z_quantize(0)
+        interleave(SCALAR, "w0", LEFT)
+        interleave(VECTOR, "x2", RIGHT)
+        z_quantize(1)
+        bb_matmul(0, 3)
+        bb_matmul(0, 1)
+        quantize("x2")
+        copy_bb_sum(0, 3)
+        interleave(VECTOR, "w0", RIGHT)
+        z_matmul(2)
+        z_copy(VECTOR, 3)
+        quantize("w0")
+        transpose_bias()
+        w_matmul(0, 0)
+        interleave(VECTOR, "w1", WHOLE)
+        copy_bb_sum(0, 1)
+        z_quantize(3)
+        z_copy(SCALAR, 2)
+        w_matmul(0, 1)
+        bb_matmul(0, 2)
+        quantize("w1")
+        bb_matmul(0, 0)
+        w_matmul(0, 3)
+        copy_w_sum(0, 0)
+        copy_bb_sum(0, 2)
+        add_w_sum(0, 1)
+        z_quantize(2)
+        w_matmul(1, 0)
+        add_bb_sum(0, 0)
+        w_matmul(0, 2)
+        bb_matmul(1, 1)
+        copy_w_sum(1, 0)
+        bb_matmul(1, 0)
+        add_w_sum(0, 3)
+        w_matmul(1, 3)
+        w_matmul(1, 1)
+        w_matmul(1, 2)
+        copy_bb_sum(1, 1)
+        bb_matmul(1, 3)
+        add_w_sum(0, 2)
+        add_bb_sum(1, 0)
+        copy_w_sum(1, 3)
+        copy_w_sum(1, 2)
+        add_w_sum(1, 1)
+        add_bb_sum(1, 3)
+        bb_matmul(1, 2)
+        add_bb_sum(1, 2, store_halves=True)

@@ -24,7 +24,7 @@ QUAD = 32
 WHOLE_BANKS = 4
 ROW_SETS = 2
 
-VECTOR, SCALAR = "vector", "scalar"
+VECTOR, SCALAR, GPSIMD = "vector", "scalar", "gpsimd"
 LEFT, RIGHT, WHOLE = slice(0, GROUP // 2), slice(GROUP // 2, GROUP), slice(0, GROUP)
 
 
@@ -34,13 +34,9 @@ def tile_rows_lora_bias_kernel(tc, x, w, a, bb, b, out):
         keep = ctx.enter_context(tc.tile_pool(name="keep", bufs=1))
         psum = ctx.enter_context(tc.psum_pool(name="psum", bufs=1))
 
-        raw_tiles = {name: keep.tile([P, PACK, GROUP], F32, name="raw_" + name, align_bytes=64)
-                     for name in ("bb", "a", "w0", "w1")}
-        raw_x = [keep.tile([P, PACK, 2 * GROUP], F32, name="raw_x%d" % pair, align_bytes=64) for pair in range(2)]
-        raw = {name: tile[:] for name, tile in raw_tiles.items()}
-        for c in range(4):
-            raw["x%d" % c] = raw_x[c // 2][:, :, GROUP * (c % 2):GROUP * (c % 2 + 1)]
-        grouped = {name: keep.tile([P, GROUP * PACK], BF16, name="grouped_" + name, align_bytes=64) for name in raw}
+        raw = {}
+        names = ("bb", "a", "w0", "w1", "x0", "x1", "x2", "x3")
+        grouped = {name: keep.tile([P, GROUP * PACK], BF16, name="grouped_" + name, align_bytes=64) for name in names}
         plain = ("w0", "w1", "x0", "x1", "x2", "x3")
         codes = {name: keep.tile([P, GROUP], U32, name="codes_" + name, align_bytes=256) for name in plain}
         scales = {name: keep.tile([P, GROUP], U8, name="scales_" + name, align_bytes=256) for name in plain}
@@ -51,10 +47,8 @@ def tile_rows_lora_bias_kernel(tc, x, w, a, bb, b, out):
         z_grouped = [keep.tile([P, COLS * PACK], BF16, name="z_grouped%d" % c, align_bytes=64) for c in range(4)]
         z_codes = [keep.tile([P, COLS], U32, name="z_codes%d" % c, align_bytes=256) for c in range(4)]
         z_scales = [keep.tile([P, COLS], U8, name="z_scales%d" % c, align_bytes=256) for c in range(4)]
-        y = {(pair, t): keep.tile([P, 2 * GROUP], F32, name="y%d%d" % (pair, t), align_bytes=64)
-             for pair in range(2) for t in range(4)}
-        bias = keep.tile([P, QUAD], F32, name="bias", align_bytes=64)
-        bias_rows = keep.tile([P, QUAD], F32, name="bias_rows", align_bytes=64)
+        bias = keep.tile([P, P], F32, name="bias", align_bytes=64)
+        bias_rows = keep.tile([P, P], F32, name="bias_rows", align_bytes=64)
         table_in = keep.tile([P, 1], F32, name="table_in")
         table_out = keep.tile([P, 1], F32, name="table_out")
 
@@ -63,9 +57,39 @@ def tile_rows_lora_bias_kernel(tc, x, w, a, bb, b, out):
                      for i in range(ROW_SETS)]
         whole_bank_of = {}
         row_banks_of = {}
+        y = [keep.tile([P, 4, 2 * GROUP], F32, name="y%d" % pair, align_bytes=64) for pair in range(2)]
+        extra = keep.tile([P, 2, 2 * GROUP], F32, name="extra", align_bytes=64)
+
+        bb_rows = bb.rearrange("(p j) m -> p j m", j=PACK)
+        x_rows = x.rearrange("(p j) n -> p j n", j=PACK)
+        w_rows = w.rearrange("(p j) m -> p j m", j=PACK)
+
+        def load(prefix, rows, first, count):
+            tile = keep.tile([P, PACK, count * GROUP], F32, name="raw_%s%d" % (prefix, first), align_bytes=64)
+            nc.sync.dma_start(out=tile[:], in_=rows[:, :, GROUP * first:GROUP * (first + count)])
+            for i in range(count):
+                raw["%s%d" % (prefix, first + i)] = tile[:, :, GROUP * i:GROUP * (i + 1)]
+
+        def load_a():
+            tile = keep.tile([P, PACK, GROUP], F32, name="raw_a", align_bytes=64)
+            nc.sync.dma_start(out=tile[:], in_=a.rearrange("(p j) r -> p j r", j=PACK))
+            raw["a"] = tile[:]
+
+        raw_bb = keep.tile([P, PACK, GROUP], F32, name="raw_bb", align_bytes=64)
+        raw["bb"] = raw_bb[:]
+
+        def load_bb_lower():
+            nc.sync.dma_start(out=raw_bb[0:ROWS], in_=bb_rows[:, :, 0:GROUP])
+
+        def load_bb_upper(engine):
+            engine.dma_start(out=raw_bb[ROWS:P], in_=bb_rows[:, :, GROUP:M])
+
+        def load_bias():
+            nc.scalar.dma_start(out=bias_rows[0:P:QUAD, :].rearrange("q (t j) -> q t j", j=QUAD),
+                                in_=b.rearrange("(t q j) o -> q t (j o)", t=4, q=P // QUAD))
 
         def by_half(tile_columns):
-            return tile_columns.rearrange("p (c half n) -> p half c n", c=2, half=2)
+            return tile_columns.rearrange("p (i half n) -> p half i n", n=COLS, half=2)
 
         def interleave(engine, name, cols):
             dst = grouped[name][:].rearrange("p (c j) -> p c j", j=PACK)[:, cols]
@@ -76,9 +100,13 @@ def tile_rows_lora_bias_kernel(tc, x, w, a, bb, b, out):
             else:
                 nc.scalar.copy(out=dst, in_=src)
 
-        def interleave_a():
-            nc.vector.tensor_copy(out=grouped["a"][:].rearrange("p (s q j) -> p q s j", s=PACK, j=PACK),
-                                  in_=raw["a"].rearrange("p j (q s) -> p q s j", s=PACK))
+        def interleave_a(engine=VECTOR):
+            dst = grouped["a"][:].rearrange("p (s q j) -> p q s j", s=PACK, j=PACK)
+            src = raw["a"].rearrange("p j (q s) -> p q s j", s=PACK)
+            if engine == VECTOR:
+                nc.vector.tensor_copy(out=dst, in_=src)
+            else:
+                nc.scalar.copy(out=dst, in_=src)
 
         def quantize(name):
             nc.vector.quantize_mx(out=codes[name][:].bitcast(FP8X4), scales=scales[name][:], in_=grouped[name][:])
@@ -93,12 +121,15 @@ def tile_rows_lora_bias_kernel(tc, x, w, a, bb, b, out):
             nc.vector.quantize_mx(out=bb_own[:, 0:GROUP].bitcast(FP8X4), scales=bb_own[:, GROUP:].bitcast(U8),
                                   in_=grouped["bb"][:])
 
-        def exchange_bb_halves():
-            nc.scalar.dma_start(out=bb_other[0:ROWS, :].bitcast(I32), in_=bb_own[ROWS:P, :].bitcast(I32))
-            nc.scalar.dma_start(out=bb_other[ROWS:P, :].bitcast(I32), in_=bb_own[0:ROWS, :].bitcast(I32))
+        def exchange_bb_halves(engine=nc.scalar):
+            engine.dma_start(out=bb_other[ROWS:P, :].bitcast(I32), in_=bb_own[0:ROWS, :].bitcast(I32))
+            engine.dma_start(out=bb_other[0:ROWS, :].bitcast(I32), in_=bb_own[ROWS:P, :].bitcast(I32))
 
         def transpose_bias():
             nc.vector.transpose(out=bias[:], in_=bias_rows[:])
+
+        def bias_of(t):
+            return bias[:, QUAD * t:QUAD * t + 1]
 
         def warm_up():
             bank = whole_banks[len(whole_bank_of) % WHOLE_BANKS]
@@ -136,20 +167,36 @@ def tile_rows_lora_bias_kernel(tc, x, w, a, bb, b, out):
             whole_bank_of[(pair, t)] = bank
             w_name = "w%d" % (t // 2)
             m_cols = slice(P * (t % 2), P * (t % 2 + 1))
-            for i in range(2 * GROUP // COLS):
+            for i in range(4):
                 x_name = "x%d" % (2 * pair + i // 2)
                 cols = slice(COLS * (i % 2), COLS * (i % 2 + 1))
                 nc.tensor.matmul_mx(out=bank[:, COLS * i:COLS * (i + 1)], lhsT=codes[w_name][:, m_cols].bitcast(FP8X4),
                                     lhsT_scale=scales[w_name][:, m_cols], rhs=codes[x_name][:, cols].bitcast(FP8X4),
                                     rhs_scale=scales[x_name][:, cols], start=True, stop=True)
 
-        def bb_matmul(pair, t):
-            banks = row_banks[len(row_banks_of) % ROW_SETS]
-            row_banks_of[(pair, t)] = banks
-            m_cols = slice(P * (t % 2), P * (t % 2 + 1))
-            m_scale_words = slice(GROUP + P // 4 * (t % 2), GROUP + P // 4 * (t % 2 + 1))
-            for i in range(2):
-                c = 2 * pair + i
+        def of_chunk(c):
+            return tuple((c, t) for t in range(4))
+
+        def of_rows(pair, u):
+            return tuple((2 * pair + i, t) for t in (2 * u, 2 * u + 1) for i in range(2))
+
+        def y_half(blocks, half, tile=None):
+            c, t = blocks[0]
+            if blocks[1][0] == c:
+                first = GROUP * (c % 2) + COLS * half
+                return y[c // 2][:, t:t + len(blocks), first:first + COLS]
+            rows = y[c // 2][:, t:t + len(blocks) // 2, :] if tile is None else tile
+            return rows.rearrange("p t (i half n) -> p half (t i) n", i=2, half=2)[:, half]
+
+        def bb_matmul(blocks):
+            banks = row_banks[len(row_banks_of) // 3 % ROW_SETS]
+            row_banks_of[blocks] = [bank[:] for bank in banks]
+            row_banks_of[blocks[0:2]] = [bank[:, 0:2, :] for bank in banks]
+            row_banks_of[blocks[2:4]] = [bank[:, 2:4, :] for bank in banks]
+            for i in range(4):
+                c, t = blocks[i]
+                m_cols = slice(P * (t % 2), P * (t % 2 + 1))
+                m_scale_words = slice(GROUP + P // 4 * (t % 2), GROUP + P // 4 * (t % 2 + 1))
                 for half in range(2):
                     rows = slice(ROWS * half, ROWS * (half + 1))
                     bb_tile = bb_own if t // 2 == half else bb_other
@@ -161,119 +208,114 @@ def tile_rows_lora_bias_kernel(tc, x, w, a, bb, b, out):
         def out_tile(pair, t):
             return out[P * t:P * (t + 1), 2 * GROUP * pair:2 * GROUP * (pair + 1)]
 
+        def store(pair, t):
+            nc.sync.dma_start(out=out_tile(pair, t), in_=y[pair][:, t, :])
+
         def copy_w_sum(pair, t):
-            nc.scalar.activation(out=y[(pair, t)][:], in_=whole_bank_of[(pair, t)][:], func=IDENTITY,
-                                 bias=bias[:, t:t + 1])
+            nc.scalar.activation(out=y[pair][:, t, :], in_=whole_bank_of[(pair, t)][:], func=IDENTITY, bias=bias_of(t))
 
         def add_bb_sum(pair, t, store_halves=False):
+            blocks = ((2 * pair, t), (2 * pair + 1, t))
             for half in range(2):
-                part = by_half(y[(pair, t)][:])[:, half]
-                nc.vector.tensor_tensor(out=part, in0=row_banks_of[(pair, t)][half][:, 0:2, :], in1=part, op=ADD)
+                part = y_half(blocks, half)
+                nc.vector.tensor_tensor(out=part, in0=row_banks_of[blocks][half], in1=part, op=ADD)
                 if store_halves:
-                    nc.sync.dma_start(out=by_half(out_tile(pair, t))[:, half], in_=part)
+                    nc.sync.dma_start(out=out_tile(pair, t).rearrange("p (i half n) -> p half i n", i=2, half=2)[:, half],
+                                      in_=part)
             if not store_halves:
-                nc.sync.dma_start(out=out_tile(pair, t), in_=y[(pair, t)][:])
+                store(pair, t)
 
-        def copy_bb_sum(pair, t):
+        def copy_bb_sum(blocks):
             for half in range(2):
-                nc.scalar.copy(out=by_half(y[(pair, t)][:])[:, half], in_=row_banks_of[(pair, t)][half][:, 0:2, :])
+                nc.scalar.copy(out=y_half(blocks, half), in_=row_banks_of[blocks][half])
 
         def add_w_sum(pair, t):
-            nc.vector.scalar_tensor_tensor(out=y[(pair, t)][:], in0=whole_bank_of[(pair, t)][:],
-                                           scalar=bias[:, t:t + 1], in1=y[(pair, t)][:], op0=ADD, op1=ADD)
-            nc.sync.dma_start(out=out_tile(pair, t), in_=y[(pair, t)][:])
+            nc.vector.scalar_tensor_tensor(out=y[pair][:, t, :], in0=whole_bank_of[(pair, t)][:],
+                                           scalar=bias_of(t), in1=y[pair][:, t, :], op0=ADD, op1=ADD)
+            store(pair, t)
+
+        def copy_w_sum_aside(pair, t, slot):
+            nc.scalar.activation(out=extra[:, slot, :], in_=whole_bank_of[(pair, t)][:], func=IDENTITY, bias=bias_of(t))
+
+        def add_on_gpsimd(pair, t, slot):
+            nc.gpsimd.tensor_tensor(out=y[pair][:, t, :], in0=y[pair][:, t, :], in1=extra[:, slot, :], op=ADD)
+            store(pair, t)
 
         ctx.enter_context(tc.manual_schedule())
 
-        bb_rows = bb.rearrange("(p j) m -> p j m", j=PACK)
-        x_rows = x.rearrange("(p j) n -> p j n", j=PACK)
-        w_rows = w.rearrange("(p j) m -> p j m", j=PACK)
-        nc.sync.dma_start(out=raw_tiles["bb"][0:ROWS], in_=bb_rows[:, :, 0:GROUP])
-        nc.scalar.dma_start(out=raw_tiles["bb"][ROWS:P], in_=bb_rows[:, :, GROUP:M])
-        nc.sync.dma_start(out=raw["a"], in_=a.rearrange("(p j) r -> p j r", j=PACK))
-        nc.sync.dma_start(out=raw_x[0][:], in_=x_rows[:, :, 0:N // 2])
-        nc.sync.dma_start(out=raw_x[1][:], in_=x_rows[:, :, N // 2:N])
-        nc.sync.dma_start(out=raw["w0"], in_=w_rows[:, :, 0:GROUP])
-        nc.sync.dma_start(out=raw["w1"], in_=w_rows[:, :, GROUP:M])
-
+        load_a()
+        load("x", x_rows, 0, 2)
+        load("x", x_rows, 2, 2)
+        load_bb_lower()
+        load("w", w_rows, 0, 1)
+        load("w", w_rows, 1, 1)
         nc.vector.memset(table_in[:], 0.0)
+        nc.vector.memset(bias_rows[:], 0.0)
+        load_bias()
         nc.scalar.activation(out=table_out[:], in_=table_in[:], func=IDENTITY)
-
-        nc.gpsimd.memset(bias_rows[:], 0.0)
-        b_rows = b.rearrange("(t q j) o -> q t (j o)", t=4, q=P // QUAD)
-        for q in range(P // QUAD):
-            nc.gpsimd.dma_start(out=bias_rows[QUAD * q:QUAD * q + 4, :], in_=b_rows[q])
-
         nc.vector.memset(bb_own[:, GROUP:], 0)
         nc.vector.memset(a_codes[:], 0)
         nc.vector.memset(a_scales[:].bitcast(U32), 0)
 
-        interleave(VECTOR, "bb", LEFT)
-        interleave(SCALAR, "bb", RIGHT)
         interleave_a()
         quantize_a()
-        warm_up()
         interleave(VECTOR, "x0", WHOLE)
+        interleave(SCALAR, "x1", RIGHT)
+        load_bb_upper(nc.scalar)
         interleave(VECTOR, "x1", LEFT)
         quantize("x0")
-        quantize_bb()
-        interleave(SCALAR, "x1", RIGHT)
-        warm_up()
-        warm_up()
         z_matmul(0)
         quantize("x1")
-        exchange_bb_halves()
         z_matmul(1)
+        interleave(VECTOR, "x2", WHOLE)
+        interleave(SCALAR, "x3", RIGHT)
+        interleave(VECTOR, "x3", LEFT)
+        quantize("x2")
+        z_matmul(2)
         z_copy(SCALAR, 0)
-        z_copy(SCALAR, 1)
-        interleave(VECTOR, "x3", WHOLE)
-        interleave(VECTOR, "x2", LEFT)
+        interleave(VECTOR, "bb", LEFT)
+        interleave(SCALAR, "bb", RIGHT)
         quantize("x3")
         z_matmul(3)
         z_quantize(0)
-        interleave(SCALAR, "w0", LEFT)
-        interleave(VECTOR, "x2", RIGHT)
-        z_quantize(1)
-        bb_matmul(0, 3)
-        bb_matmul(0, 1)
-        quantize("x2")
-        copy_bb_sum(0, 3)
-        interleave(VECTOR, "w0", RIGHT)
-        z_matmul(2)
-        z_copy(VECTOR, 3)
-        quantize("w0")
-        transpose_bias()
-        w_matmul(0, 0)
-        interleave(VECTOR, "w1", WHOLE)
-        copy_bb_sum(0, 1)
-        z_quantize(3)
+        quantize_bb()
+        exchange_bb_halves(nc.sync)
+        z_copy(SCALAR, 1)
         z_copy(SCALAR, 2)
+        z_copy(SCALAR, 3)
+        interleave(VECTOR, "w0", WHOLE)
+        z_quantize(1)
+        transpose_bias()
+        quantize("w0")
+        w_matmul(0, 0)
         w_matmul(0, 1)
-        bb_matmul(0, 2)
-        quantize("w1")
-        bb_matmul(0, 0)
-        w_matmul(0, 3)
-        copy_w_sum(0, 0)
-        copy_bb_sum(0, 2)
-        add_w_sum(0, 1)
         z_quantize(2)
+        interleave(VECTOR, "w1", WHOLE)
+        z_quantize(3)
+        quantize("w1")
+        bb_matmul(of_rows(0, 0))
         w_matmul(1, 0)
-        add_bb_sum(0, 0)
-        w_matmul(0, 2)
-        bb_matmul(1, 1)
-        copy_w_sum(1, 0)
-        bb_matmul(1, 0)
-        add_w_sum(0, 3)
-        w_matmul(1, 3)
         w_matmul(1, 1)
+        bb_matmul(of_rows(1, 0))
+        copy_w_sum(0, 0)
+        w_matmul(0, 2)
+        copy_w_sum(0, 1)
+        w_matmul(0, 3)
+        add_bb_sum(0, 0)
+        copy_w_sum(1, 0)
+        add_bb_sum(0, 1)
+        bb_matmul(of_rows(0, 1))
         w_matmul(1, 2)
-        copy_bb_sum(1, 1)
-        bb_matmul(1, 3)
-        add_w_sum(0, 2)
+        copy_w_sum(1, 1)
+        w_matmul(1, 3)
         add_bb_sum(1, 0)
-        copy_w_sum(1, 3)
+        copy_w_sum(0, 2)
+        add_bb_sum(1, 1)
+        bb_matmul(of_rows(1, 1))
+        copy_w_sum(0, 3)
         copy_w_sum(1, 2)
-        add_w_sum(1, 1)
+        copy_w_sum(1, 3)
+        add_bb_sum(0, 2)
+        add_bb_sum(0, 3)
+        add_bb_sum(1, 2)
         add_bb_sum(1, 3)
-        bb_matmul(1, 2)
-        add_bb_sum(1, 2, store_halves=True)

@@ -36,14 +36,14 @@ def tile_rows_lora_bias_kernel(tc, x, w, a, bb, b, out):
 
         raw = {}
         names = ("bb", "a", "w0", "w1", "x0", "x1", "x2", "x3")
-        grouped = {name: keep.tile([P, GROUP * PACK], BF16, name="grouped_" + name, align_bytes=64) for name in names}
+        grouped = {name: keep.tile([P, (M if name == "bb" else GROUP) * PACK], BF16, name="grouped_" + name, align_bytes=64)
+                   for name in names}
         plain = ("w0", "w1", "x0", "x1", "x2", "x3")
         codes = {name: keep.tile([P, GROUP], U32, name="codes_" + name, align_bytes=256) for name in plain}
         scales = {name: keep.tile([P, GROUP], U8, name="scales_" + name, align_bytes=256) for name in plain}
         a_codes = keep.tile([P, 9 * ROWS], U32, name="a_codes", align_bytes=256)
         a_scales = keep.tile([P, 9 * ROWS], U8, name="a_scales", align_bytes=256)
-        bb_own = keep.tile([P, GROUP + SCALE_WORDS], U32, name="bb_own", align_bytes=256)
-        bb_other = keep.tile([P, GROUP + SCALE_WORDS], U32, name="bb_other", align_bytes=256)
+        bb_packed = keep.tile([P, M + M // 4], U32, name="bb_packed", align_bytes=256)
         z_grouped = [keep.tile([P, COLS * PACK], BF16, name="z_grouped%d" % c, align_bytes=64) for c in range(4)]
         z_codes = [keep.tile([P, COLS], U32, name="z_codes%d" % c, align_bytes=256) for c in range(4)]
         z_scales = [keep.tile([P, COLS], U8, name="z_scales%d" % c, align_bytes=256) for c in range(4)]
@@ -58,7 +58,6 @@ def tile_rows_lora_bias_kernel(tc, x, w, a, bb, b, out):
         whole_bank_of = {}
         row_banks_of = {}
         y = [keep.tile([P, 4, 2 * GROUP], F32, name="y%d" % pair, align_bytes=64) for pair in range(2)]
-        extra = keep.tile([P, 2, 2 * GROUP], F32, name="extra", align_bytes=64)
 
         bb_rows = bb.rearrange("(p j) m -> p j m", j=PACK)
         x_rows = x.rearrange("(p j) n -> p j n", j=PACK)
@@ -75,18 +74,15 @@ def tile_rows_lora_bias_kernel(tc, x, w, a, bb, b, out):
             nc.sync.dma_start(out=tile[:], in_=a.rearrange("(p j) r -> p j r", j=PACK))
             raw["a"] = tile[:]
 
-        raw_bb = keep.tile([P, PACK, GROUP], F32, name="raw_bb", align_bytes=64)
+        raw_bb = keep.tile([P, PACK, M], F32, name="raw_bb", align_bytes=64)
         raw["bb"] = raw_bb[:]
 
-        def load_bb_lower():
-            nc.sync.dma_start(out=raw_bb[0:ROWS], in_=bb_rows[:, :, 0:GROUP])
-
-        def load_bb_upper(engine):
-            engine.dma_start(out=raw_bb[ROWS:P], in_=bb_rows[:, :, GROUP:M])
+        def load_bb():
+            nc.sync.dma_start(out=raw_bb[QUAD:QUAD + ROWS], in_=bb_rows)
 
         def load_bias():
-            nc.scalar.dma_start(out=bias_rows[0:P:QUAD, :].rearrange("q (t j) -> q t j", j=QUAD),
-                                in_=b.rearrange("(t q j) o -> q t (j o)", t=4, q=P // QUAD))
+            nc.sync.dma_start(out=bias_rows[0:P:QUAD, :].rearrange("q (t j) -> q t j", j=QUAD),
+                              in_=b.rearrange("(t q j) o -> q t (j o)", t=4, q=P // QUAD))
 
         def by_half(tile_columns):
             return tile_columns.rearrange("p (i half n) -> p half i n", n=COLS, half=2)
@@ -101,12 +97,10 @@ def tile_rows_lora_bias_kernel(tc, x, w, a, bb, b, out):
                 nc.scalar.copy(out=dst, in_=src)
 
         def interleave_a(engine=VECTOR):
-            dst = grouped["a"][:].rearrange("p (s q j) -> p q s j", s=PACK, j=PACK)
-            src = raw["a"].rearrange("p j (q s) -> p q s j", s=PACK)
-            if engine == VECTOR:
-                nc.vector.tensor_copy(out=dst, in_=src)
-            else:
-                nc.scalar.copy(out=dst, in_=src)
+            dst = grouped["a"][:].rearrange("p (s g q j) -> p g q s j", s=PACK, g=2, j=PACK)
+            src = raw["a"].rearrange("p j (g q s) -> p g q s j", g=2, s=PACK)
+            for g in range(2):
+                nc.vector.tensor_copy(out=dst[:, 1 - g], in_=src[:, g])
 
         def quantize(name):
             nc.vector.quantize_mx(out=codes[name][:].bitcast(FP8X4), scales=scales[name][:], in_=grouped[name][:])
@@ -118,12 +112,12 @@ def tile_rows_lora_bias_kernel(tc, x, w, a, bb, b, out):
                                       in_=grouped["a"][:, ROWS * PACK * s:ROWS * PACK * (s + 1)])
 
         def quantize_bb():
-            nc.vector.quantize_mx(out=bb_own[:, 0:GROUP].bitcast(FP8X4), scales=bb_own[:, GROUP:].bitcast(U8),
+            nc.vector.quantize_mx(out=bb_packed[:, 0:M].bitcast(FP8X4), scales=bb_packed[:, M:].bitcast(U8),
                                   in_=grouped["bb"][:])
 
-        def exchange_bb_halves(engine=nc.scalar):
-            engine.dma_start(out=bb_other[ROWS:P, :].bitcast(I32), in_=bb_own[0:ROWS, :].bitcast(I32))
-            engine.dma_start(out=bb_other[0:ROWS, :].bitcast(I32), in_=bb_own[ROWS:P, :].bitcast(I32))
+        def spread_bb():
+            nc.sync.dma_start(out=bb_packed[3 * QUAD:P, :].bitcast(I32), in_=bb_packed[QUAD:2 * QUAD, :].bitcast(I32))
+            nc.sync.dma_start(out=bb_packed[0:QUAD, :].bitcast(I32), in_=bb_packed[2 * QUAD:3 * QUAD, :].bitcast(I32))
 
         def transpose_bias():
             nc.vector.transpose(out=bias[:], in_=bias_rows[:])
@@ -195,13 +189,12 @@ def tile_rows_lora_bias_kernel(tc, x, w, a, bb, b, out):
             row_banks_of[blocks[2:4]] = [bank[:, 2:4, :] for bank in banks]
             for i in range(4):
                 c, t = blocks[i]
-                m_cols = slice(P * (t % 2), P * (t % 2 + 1))
-                m_scale_words = slice(GROUP + P // 4 * (t % 2), GROUP + P // 4 * (t % 2 + 1))
+                m_cols = slice(P * t, P * (t + 1))
+                m_scale_words = slice(M + P // 4 * t, M + P // 4 * (t + 1))
                 for half in range(2):
                     rows = slice(ROWS * half, ROWS * (half + 1))
-                    bb_tile = bb_own if t // 2 == half else bb_other
-                    nc.tensor.matmul_mx(out=banks[half][:, i, :], lhsT=bb_tile[rows, m_cols].bitcast(FP8X4),
-                                        lhsT_scale=bb_tile[rows, m_scale_words].bitcast(U8),
+                    nc.tensor.matmul_mx(out=banks[half][:, i, :], lhsT=bb_packed[rows, m_cols].bitcast(FP8X4),
+                                        lhsT_scale=bb_packed[rows, m_scale_words].bitcast(U8),
                                         rhs=z_codes[c][rows, :].bitcast(FP8X4), rhs_scale=z_scales[c][rows, :],
                                         start=True, stop=True)
 
@@ -234,26 +227,20 @@ def tile_rows_lora_bias_kernel(tc, x, w, a, bb, b, out):
                                            scalar=bias_of(t), in1=y[pair][:, t, :], op0=ADD, op1=ADD)
             store(pair, t)
 
-        def copy_w_sum_aside(pair, t, slot):
-            nc.scalar.activation(out=extra[:, slot, :], in_=whole_bank_of[(pair, t)][:], func=IDENTITY, bias=bias_of(t))
-
-        def add_on_gpsimd(pair, t, slot):
-            nc.gpsimd.tensor_tensor(out=y[pair][:, t, :], in0=y[pair][:, t, :], in1=extra[:, slot, :], op=ADD)
-            store(pair, t)
-
         ctx.enter_context(tc.manual_schedule())
 
         load_a()
         load("x", x_rows, 0, 2)
+        nc.vector.memset(bias_rows[:], 0.0)
+        nc.vector.memset(raw_bb[:], 0.0)
+        load_bias()
+        load_bb()
         load("x", x_rows, 2, 2)
-        load_bb_lower()
         load("w", w_rows, 0, 1)
         load("w", w_rows, 1, 1)
         nc.vector.memset(table_in[:], 0.0)
-        nc.vector.memset(bias_rows[:], 0.0)
-        load_bias()
         nc.scalar.activation(out=table_out[:], in_=table_in[:], func=IDENTITY)
-        nc.vector.memset(bb_own[:, GROUP:], 0)
+        nc.vector.memset(bb_packed[:, M:], 0)
         nc.vector.memset(a_codes[:], 0)
         nc.vector.memset(a_scales[:].bitcast(U32), 0)
 
@@ -261,61 +248,63 @@ def tile_rows_lora_bias_kernel(tc, x, w, a, bb, b, out):
         quantize_a()
         interleave(VECTOR, "x0", WHOLE)
         interleave(SCALAR, "x1", RIGHT)
-        load_bb_upper(nc.scalar)
         interleave(VECTOR, "x1", LEFT)
         quantize("x0")
         z_matmul(0)
         quantize("x1")
         z_matmul(1)
+        warm_up()
+        warm_up()
+        interleave(SCALAR, "bb", slice(352, 512))
+        interleave(VECTOR, "bb", slice(0, 352))
+        transpose_bias()
+        quantize_bb()
+        spread_bb()
+        z_copy(SCALAR, 0)
         interleave(VECTOR, "x2", WHOLE)
         interleave(SCALAR, "x3", RIGHT)
+        z_copy(SCALAR, 1)
         interleave(VECTOR, "x3", LEFT)
         quantize("x2")
         z_matmul(2)
-        z_copy(SCALAR, 0)
-        interleave(VECTOR, "bb", LEFT)
-        interleave(SCALAR, "bb", RIGHT)
         quantize("x3")
         z_matmul(3)
+        interleave(SCALAR, "w0", RIGHT)
+        interleave(VECTOR, "w0", LEFT)
         z_quantize(0)
-        quantize_bb()
-        exchange_bb_halves(nc.sync)
-        z_copy(SCALAR, 1)
+        z_quantize(1)
         z_copy(SCALAR, 2)
         z_copy(SCALAR, 3)
-        interleave(VECTOR, "w0", WHOLE)
-        z_quantize(1)
-        transpose_bias()
         quantize("w0")
         w_matmul(0, 0)
         w_matmul(0, 1)
-        z_quantize(2)
         interleave(VECTOR, "w1", WHOLE)
-        z_quantize(3)
+        z_quantize(2)
         quantize("w1")
+        z_quantize(3)
         bb_matmul(of_rows(0, 0))
-        w_matmul(1, 0)
-        w_matmul(1, 1)
-        bb_matmul(of_rows(1, 0))
-        copy_w_sum(0, 0)
-        w_matmul(0, 2)
-        copy_w_sum(0, 1)
-        w_matmul(0, 3)
-        add_bb_sum(0, 0)
-        copy_w_sum(1, 0)
-        add_bb_sum(0, 1)
         bb_matmul(of_rows(0, 1))
+        copy_w_sum(0, 0)
+        copy_w_sum(0, 1)
+        w_matmul(1, 0)
+        w_matmul(0, 2)
+        w_matmul(0, 3)
         w_matmul(1, 2)
-        copy_w_sum(1, 1)
+        add_bb_sum(0, 0)
+        add_bb_sum(0, 1)
+        copy_bb_sum(of_rows(0, 1)[0:2])
+        copy_bb_sum(of_rows(0, 1)[2:4])
+        bb_matmul(of_rows(1, 0))
+        bb_matmul(of_rows(1, 1))
+        add_w_sum(0, 2)
+        add_w_sum(0, 3)
+        copy_w_sum(1, 0)
+        copy_w_sum(1, 2)
+        w_matmul(1, 1)
         w_matmul(1, 3)
         add_bb_sum(1, 0)
-        copy_w_sum(0, 2)
-        add_bb_sum(1, 1)
-        bb_matmul(of_rows(1, 1))
-        copy_w_sum(0, 3)
-        copy_w_sum(1, 2)
-        copy_w_sum(1, 3)
-        add_bb_sum(0, 2)
-        add_bb_sum(0, 3)
+        copy_bb_sum(of_rows(1, 0)[2:4])
         add_bb_sum(1, 2)
-        add_bb_sum(1, 3)
+        copy_bb_sum(of_rows(1, 1)[2:4])
+        add_w_sum(1, 1)
+        add_w_sum(1, 3)

@@ -49,8 +49,6 @@ def tile_rows_lora_bias_kernel(tc, x, w, a, bb, b, out):
         z_scales = [keep.tile([P, COLS], U8, name="z_scales%d" % c, align_bytes=256) for c in range(4)]
         bias = keep.tile([P, P], F32, name="bias", align_bytes=64)
         bias_rows = keep.tile([P, P], F32, name="bias_rows", align_bytes=64)
-        table_in = keep.tile([P, 1], F32, name="table_in")
-        table_out = keep.tile([P, 1], F32, name="table_out")
 
         whole_banks = [psum.tile([P, PACK * COLS], F32, name="whole_bank%d" % i) for i in range(WHOLE_BANKS)]
         row_banks = [[psum.tile([P, PACK, COLS], F32, name="row_bank%d%d" % (half, i)) for half in range(2)]
@@ -227,6 +225,26 @@ def tile_rows_lora_bias_kernel(tc, x, w, a, bb, b, out):
                                            scalar=bias_of(t), in1=y[pair][:, t, :], op0=ADD, op1=ADD)
             store(pair, t)
 
+        def finish_by_chunk(pair, t):
+            blocks = ((2 * pair, t), (2 * pair + 1, t))
+            for i in range(2):
+                cols = slice(GROUP * i, GROUP * (i + 1))
+                nc.scalar.activation(out=y[pair][:, t, cols], in_=whole_bank_of[(pair, t)][:, cols], func=IDENTITY,
+                                     bias=bias_of(t))
+            for i in range(2):
+                cols = slice(GROUP * i, GROUP * (i + 1))
+                for half in range(2):
+                    part = y_half(blocks, half)[:, i]
+                    nc.vector.tensor_tensor(out=part, in0=row_banks_of[blocks][half][:, i], in1=part, op=ADD)
+                nc.sync.dma_start(out=out_tile(pair, t)[:, cols], in_=y[pair][:, t, cols])
+
+        def add_w_sum_by_chunk(pair, t):
+            for i in range(2):
+                cols = slice(GROUP * i, GROUP * (i + 1))
+                nc.vector.scalar_tensor_tensor(out=y[pair][:, t, cols], in0=whole_bank_of[(pair, t)][:, cols],
+                                               scalar=bias_of(t), in1=y[pair][:, t, cols], op0=ADD, op1=ADD)
+                nc.sync.dma_start(out=out_tile(pair, t)[:, cols], in_=y[pair][:, t, cols])
+
         ctx.enter_context(tc.manual_schedule())
 
         load_a()
@@ -238,8 +256,6 @@ def tile_rows_lora_bias_kernel(tc, x, w, a, bb, b, out):
         load("x", x_rows, 2, 2)
         load("w", w_rows, 0, 1)
         load("w", w_rows, 1, 1)
-        nc.vector.memset(table_in[:], 0.0)
-        nc.scalar.activation(out=table_out[:], in_=table_in[:], func=IDENTITY)
         nc.vector.memset(bb_packed[:, M:], 0)
         nc.vector.memset(a_codes[:], 0)
         nc.vector.memset(a_scales[:].bitcast(U32), 0)
@@ -262,15 +278,15 @@ def tile_rows_lora_bias_kernel(tc, x, w, a, bb, b, out):
         spread_bb()
         z_copy(SCALAR, 0)
         interleave(VECTOR, "x2", WHOLE)
-        interleave(SCALAR, "x3", RIGHT)
+        interleave(SCALAR, "x3", slice(128, 256))
         z_copy(SCALAR, 1)
-        interleave(VECTOR, "x3", LEFT)
+        interleave(VECTOR, "x3", slice(0, 128))
         quantize("x2")
         z_matmul(2)
         quantize("x3")
         z_matmul(3)
-        interleave(SCALAR, "w0", RIGHT)
-        interleave(VECTOR, "w0", LEFT)
+        interleave(SCALAR, "w0", slice(192, 256))
+        interleave(VECTOR, "w0", slice(0, 192))
         z_quantize(0)
         z_quantize(1)
         z_copy(SCALAR, 2)
@@ -286,10 +302,10 @@ def tile_rows_lora_bias_kernel(tc, x, w, a, bb, b, out):
         bb_matmul(of_rows(0, 1))
         copy_w_sum(0, 0)
         copy_w_sum(0, 1)
-        w_matmul(1, 0)
         w_matmul(0, 2)
         w_matmul(0, 3)
-        w_matmul(1, 2)
+        w_matmul(1, 0)
+        w_matmul(1, 1)
         add_bb_sum(0, 0)
         add_bb_sum(0, 1)
         copy_bb_sum(of_rows(0, 1)[0:2])
@@ -299,12 +315,12 @@ def tile_rows_lora_bias_kernel(tc, x, w, a, bb, b, out):
         add_w_sum(0, 2)
         add_w_sum(0, 3)
         copy_w_sum(1, 0)
-        copy_w_sum(1, 2)
-        w_matmul(1, 1)
+        copy_w_sum(1, 1)
+        w_matmul(1, 2)
         w_matmul(1, 3)
         add_bb_sum(1, 0)
-        copy_bb_sum(of_rows(1, 0)[2:4])
-        add_bb_sum(1, 2)
+        add_bb_sum(1, 1)
+        copy_bb_sum(of_rows(1, 1)[0:2])
         copy_bb_sum(of_rows(1, 1)[2:4])
-        add_w_sum(1, 1)
+        add_w_sum(1, 2)
         add_w_sum(1, 3)

@@ -16,16 +16,20 @@ IDENTITY = mybir.ActivationFunctionType.Identity
 
 P = 128
 ROWS = 64
+QUAD = 32
 PACK = 4
 GROUP = 256
 COLS = 128
-SCALE_WORDS = GROUP // 4
-QUAD = 32
+STRIPS = 2 * PACK + 1
 WHOLE_BANKS = 4
 ROW_SETS = 2
 
-VECTOR, SCALAR, GPSIMD = "vector", "scalar", "gpsimd"
-LEFT, RIGHT, WHOLE = slice(0, GROUP // 2), slice(GROUP // 2, GROUP), slice(0, GROUP)
+VECTOR_X_COLS = 128
+VECTOR_BB_COLS = 352
+VECTOR_W0_COLS = 192
+
+VECTOR, SCALAR = "vector", "scalar"
+WHOLE = slice(0, GROUP)
 
 
 def tile_rows_lora_bias_kernel(tc, x, w, a, bb, b, out):
@@ -41,8 +45,8 @@ def tile_rows_lora_bias_kernel(tc, x, w, a, bb, b, out):
         plain = ("w0", "w1", "x0", "x1", "x2", "x3")
         codes = {name: keep.tile([P, GROUP], U32, name="codes_" + name, align_bytes=256) for name in plain}
         scales = {name: keep.tile([P, GROUP], U8, name="scales_" + name, align_bytes=256) for name in plain}
-        a_codes = keep.tile([P, 9 * ROWS], U32, name="a_codes", align_bytes=256)
-        a_scales = keep.tile([P, 9 * ROWS], U8, name="a_scales", align_bytes=256)
+        a_codes = keep.tile([P, STRIPS * ROWS], U32, name="a_codes", align_bytes=256)
+        a_scales = keep.tile([P, STRIPS * ROWS], U8, name="a_scales", align_bytes=256)
         bb_packed = keep.tile([P, M + M // 4], U32, name="bb_packed", align_bytes=256)
         z_grouped = [keep.tile([P, COLS * PACK], BF16, name="z_grouped%d" % c, align_bytes=64) for c in range(4)]
         z_codes = [keep.tile([P, COLS], U32, name="z_codes%d" % c, align_bytes=256) for c in range(4)]
@@ -79,11 +83,8 @@ def tile_rows_lora_bias_kernel(tc, x, w, a, bb, b, out):
             nc.sync.dma_start(out=raw_bb[QUAD:QUAD + ROWS], in_=bb_rows)
 
         def load_bias():
-            nc.sync.dma_start(out=bias_rows[0:P:QUAD, :].rearrange("q (t j) -> q t j", j=QUAD),
-                              in_=b.rearrange("(t q j) o -> q t (j o)", t=4, q=P // QUAD))
-
-        def by_half(tile_columns):
-            return tile_columns.rearrange("p (i half n) -> p half i n", n=COLS, half=2)
+            nc.gpsimd.dma_start(out=bias_rows[0:P:QUAD, :].rearrange("q (t j) -> q t j", j=QUAD),
+                                in_=b.rearrange("(t q j) o -> q t (j o)", t=4, q=P // QUAD))
 
         def interleave(engine, name, cols):
             dst = grouped[name][:].rearrange("p (c j) -> p c j", j=PACK)[:, cols]
@@ -94,7 +95,7 @@ def tile_rows_lora_bias_kernel(tc, x, w, a, bb, b, out):
             else:
                 nc.scalar.copy(out=dst, in_=src)
 
-        def interleave_a(engine=VECTOR):
+        def interleave_a():
             dst = grouped["a"][:].rearrange("p (s g q j) -> p g q s j", s=PACK, g=2, j=PACK)
             src = raw["a"].rearrange("p j (g q s) -> p g q s j", g=2, s=PACK)
             for g in range(2):
@@ -123,8 +124,11 @@ def tile_rows_lora_bias_kernel(tc, x, w, a, bb, b, out):
         def bias_of(t):
             return bias[:, QUAD * t:QUAD * t + 1]
 
+        def next_whole_bank():
+            return whole_banks[len(whole_bank_of) % WHOLE_BANKS]
+
         def warm_up():
-            bank = whole_banks[len(whole_bank_of) % WHOLE_BANKS]
+            bank = next_whole_bank()
             for s in range(PACK):
                 nc.tensor.matmul_mx(out=bank[:, COLS * s:COLS * (s + 1)], lhsT=a_codes[:, 0:P].bitcast(FP8X4),
                                     lhsT_scale=a_scales[:, 0:P], rhs=a_codes[:, 0:COLS].bitcast(FP8X4),
@@ -132,7 +136,7 @@ def tile_rows_lora_bias_kernel(tc, x, w, a, bb, b, out):
 
         def z_matmul(c):
             name = "x%d" % c
-            bank = whole_banks[len(whole_bank_of) % WHOLE_BANKS][:].rearrange("p (s n) -> p s n", s=PACK)
+            bank = next_whole_bank()[:].rearrange("p (s n) -> p s n", s=PACK)
             whole_bank_of[c] = bank
             for s in range(PACK):
                 for half in range(2):
@@ -143,19 +147,15 @@ def tile_rows_lora_bias_kernel(tc, x, w, a, bb, b, out):
                                         lhsT_scale=a_scales[:, window], rhs=codes[name][:, cols].bitcast(FP8X4),
                                         rhs_scale=scales[name][:, cols], start=(half == 0), stop=(half == 1))
 
-        def z_copy(engine, c):
-            dst = z_grouped[c][:].rearrange("p (n s) -> p n s", s=PACK)
-            src = whole_bank_of[c].rearrange("p s n -> p n s")
-            if engine == VECTOR:
-                nc.vector.tensor_copy(out=dst, in_=src)
-            else:
-                nc.scalar.copy(out=dst, in_=src)
+        def z_copy(c):
+            nc.scalar.copy(out=z_grouped[c][:].rearrange("p (n s) -> p n s", s=PACK),
+                           in_=whole_bank_of[c].rearrange("p s n -> p n s"))
 
         def z_quantize(c):
             nc.vector.quantize_mx(out=z_codes[c][:].bitcast(FP8X4), scales=z_scales[c][:], in_=z_grouped[c][:])
 
         def w_matmul(pair, t):
-            bank = whole_banks[len(whole_bank_of) % WHOLE_BANKS]
+            bank = next_whole_bank()
             whole_bank_of[(pair, t)] = bank
             w_name = "w%d" % (t // 2)
             m_cols = slice(P * (t % 2), P * (t % 2 + 1))
@@ -166,90 +166,51 @@ def tile_rows_lora_bias_kernel(tc, x, w, a, bb, b, out):
                                     lhsT_scale=scales[w_name][:, m_cols], rhs=codes[x_name][:, cols].bitcast(FP8X4),
                                     rhs_scale=scales[x_name][:, cols], start=True, stop=True)
 
-        def of_chunk(c):
-            return tuple((c, t) for t in range(4))
-
-        def of_rows(pair, u):
-            return tuple((2 * pair + i, t) for t in (2 * u, 2 * u + 1) for i in range(2))
-
-        def y_half(blocks, half, tile=None):
-            c, t = blocks[0]
-            if blocks[1][0] == c:
-                first = GROUP * (c % 2) + COLS * half
-                return y[c // 2][:, t:t + len(blocks), first:first + COLS]
-            rows = y[c // 2][:, t:t + len(blocks) // 2, :] if tile is None else tile
-            return rows.rearrange("p t (i half n) -> p half (t i) n", i=2, half=2)[:, half]
-
-        def bb_matmul(blocks):
-            banks = row_banks[len(row_banks_of) // 3 % ROW_SETS]
-            row_banks_of[blocks] = [bank[:] for bank in banks]
-            row_banks_of[blocks[0:2]] = [bank[:, 0:2, :] for bank in banks]
-            row_banks_of[blocks[2:4]] = [bank[:, 2:4, :] for bank in banks]
-            for i in range(4):
-                c, t = blocks[i]
+        def bb_matmul(pair, u):
+            banks = row_banks[len(row_banks_of) // 2 % ROW_SETS]
+            for t in (2 * u, 2 * u + 1):
+                row_banks_of[(pair, t)] = [bank[:, 2 * (t % 2):2 * (t % 2 + 1), :] for bank in banks]
                 m_cols = slice(P * t, P * (t + 1))
                 m_scale_words = slice(M + P // 4 * t, M + P // 4 * (t + 1))
-                for half in range(2):
-                    rows = slice(ROWS * half, ROWS * (half + 1))
-                    nc.tensor.matmul_mx(out=banks[half][:, i, :], lhsT=bb_packed[rows, m_cols].bitcast(FP8X4),
-                                        lhsT_scale=bb_packed[rows, m_scale_words].bitcast(U8),
-                                        rhs=z_codes[c][rows, :].bitcast(FP8X4), rhs_scale=z_scales[c][rows, :],
-                                        start=True, stop=True)
+                for i in range(2):
+                    c = 2 * pair + i
+                    for half in range(2):
+                        rows = slice(ROWS * half, ROWS * (half + 1))
+                        nc.tensor.matmul_mx(out=banks[half][:, 2 * (t % 2) + i, :],
+                                            lhsT=bb_packed[rows, m_cols].bitcast(FP8X4),
+                                            lhsT_scale=bb_packed[rows, m_scale_words].bitcast(U8),
+                                            rhs=z_codes[c][rows, :].bitcast(FP8X4), rhs_scale=z_scales[c][rows, :],
+                                            start=True, stop=True)
 
-        def out_tile(pair, t):
-            return out[P * t:P * (t + 1), 2 * GROUP * pair:2 * GROUP * (pair + 1)]
+        def y_half(pair, t, half):
+            return y[pair][:, t:t + 1, :].rearrange("p t (i half n) -> p half (t i) n", i=2, half=2)[:, half]
 
         def store(pair, t):
-            nc.sync.dma_start(out=out_tile(pair, t), in_=y[pair][:, t, :])
+            nc.sync.dma_start(out=out[P * t:P * (t + 1), 2 * GROUP * pair:2 * GROUP * (pair + 1)], in_=y[pair][:, t, :])
 
         def copy_w_sum(pair, t):
             nc.scalar.activation(out=y[pair][:, t, :], in_=whole_bank_of[(pair, t)][:], func=IDENTITY, bias=bias_of(t))
 
-        def add_bb_sum(pair, t, store_halves=False):
-            blocks = ((2 * pair, t), (2 * pair + 1, t))
+        def add_bb_sum(pair, t):
             for half in range(2):
-                part = y_half(blocks, half)
-                nc.vector.tensor_tensor(out=part, in0=row_banks_of[blocks][half], in1=part, op=ADD)
-                if store_halves:
-                    nc.sync.dma_start(out=out_tile(pair, t).rearrange("p (i half n) -> p half i n", i=2, half=2)[:, half],
-                                      in_=part)
-            if not store_halves:
-                store(pair, t)
+                part = y_half(pair, t, half)
+                nc.vector.tensor_tensor(out=part, in0=row_banks_of[(pair, t)][half], in1=part, op=ADD)
+            store(pair, t)
 
-        def copy_bb_sum(blocks):
+        def copy_bb_sum(pair, t):
             for half in range(2):
-                nc.scalar.copy(out=y_half(blocks, half), in_=row_banks_of[blocks][half])
+                nc.scalar.copy(out=y_half(pair, t, half), in_=row_banks_of[(pair, t)][half])
 
         def add_w_sum(pair, t):
             nc.vector.scalar_tensor_tensor(out=y[pair][:, t, :], in0=whole_bank_of[(pair, t)][:],
                                            scalar=bias_of(t), in1=y[pair][:, t, :], op0=ADD, op1=ADD)
             store(pair, t)
 
-        def finish_by_chunk(pair, t):
-            blocks = ((2 * pair, t), (2 * pair + 1, t))
-            for i in range(2):
-                cols = slice(GROUP * i, GROUP * (i + 1))
-                nc.scalar.activation(out=y[pair][:, t, cols], in_=whole_bank_of[(pair, t)][:, cols], func=IDENTITY,
-                                     bias=bias_of(t))
-            for i in range(2):
-                cols = slice(GROUP * i, GROUP * (i + 1))
-                for half in range(2):
-                    part = y_half(blocks, half)[:, i]
-                    nc.vector.tensor_tensor(out=part, in0=row_banks_of[blocks][half][:, i], in1=part, op=ADD)
-                nc.sync.dma_start(out=out_tile(pair, t)[:, cols], in_=y[pair][:, t, cols])
-
-        def add_w_sum_by_chunk(pair, t):
-            for i in range(2):
-                cols = slice(GROUP * i, GROUP * (i + 1))
-                nc.vector.scalar_tensor_tensor(out=y[pair][:, t, cols], in0=whole_bank_of[(pair, t)][:, cols],
-                                               scalar=bias_of(t), in1=y[pair][:, t, cols], op0=ADD, op1=ADD)
-                nc.sync.dma_start(out=out_tile(pair, t)[:, cols], in_=y[pair][:, t, cols])
-
         ctx.enter_context(tc.manual_schedule())
 
         load_a()
         load("x", x_rows, 0, 2)
-        nc.vector.memset(bias_rows[:], 0.0)
+        nc.gpsimd.memset(bias_rows[:], 0.0)
         nc.vector.memset(raw_bb[:], 0.0)
         load_bias()
         load_bb()
@@ -263,34 +224,37 @@ def tile_rows_lora_bias_kernel(tc, x, w, a, bb, b, out):
         interleave_a()
         quantize_a()
         interleave(VECTOR, "x0", WHOLE)
-        interleave(SCALAR, "x1", RIGHT)
-        interleave(VECTOR, "x1", LEFT)
+        interleave(SCALAR, "x1", slice(VECTOR_X_COLS, GROUP))
+        interleave(VECTOR, "x1", slice(0, VECTOR_X_COLS))
         quantize("x0")
         z_matmul(0)
         quantize("x1")
         z_matmul(1)
         warm_up()
         warm_up()
-        interleave(SCALAR, "bb", slice(352, 512))
-        interleave(VECTOR, "bb", slice(0, 352))
+
+        interleave(SCALAR, "bb", slice(VECTOR_BB_COLS, M))
+        interleave(VECTOR, "bb", slice(0, VECTOR_BB_COLS))
         transpose_bias()
         quantize_bb()
         spread_bb()
-        z_copy(SCALAR, 0)
+        z_copy(0)
+
         interleave(VECTOR, "x2", WHOLE)
-        interleave(SCALAR, "x3", slice(128, 256))
-        z_copy(SCALAR, 1)
-        interleave(VECTOR, "x3", slice(0, 128))
+        interleave(SCALAR, "x3", slice(VECTOR_X_COLS, GROUP))
+        z_copy(1)
+        interleave(VECTOR, "x3", slice(0, VECTOR_X_COLS))
         quantize("x2")
         z_matmul(2)
         quantize("x3")
         z_matmul(3)
-        interleave(SCALAR, "w0", slice(192, 256))
-        interleave(VECTOR, "w0", slice(0, 192))
+
+        interleave(SCALAR, "w0", slice(VECTOR_W0_COLS, GROUP))
+        interleave(VECTOR, "w0", slice(0, VECTOR_W0_COLS))
         z_quantize(0)
         z_quantize(1)
-        z_copy(SCALAR, 2)
-        z_copy(SCALAR, 3)
+        z_copy(2)
+        z_copy(3)
         quantize("w0")
         w_matmul(0, 0)
         w_matmul(0, 1)
@@ -298,29 +262,24 @@ def tile_rows_lora_bias_kernel(tc, x, w, a, bb, b, out):
         z_quantize(2)
         quantize("w1")
         z_quantize(3)
-        bb_matmul(of_rows(0, 0))
-        bb_matmul(of_rows(0, 1))
-        copy_w_sum(0, 0)
-        copy_w_sum(0, 1)
-        w_matmul(0, 2)
-        w_matmul(0, 3)
-        w_matmul(1, 0)
-        w_matmul(1, 1)
-        add_bb_sum(0, 0)
-        add_bb_sum(0, 1)
-        copy_bb_sum(of_rows(0, 1)[0:2])
-        copy_bb_sum(of_rows(0, 1)[2:4])
-        bb_matmul(of_rows(1, 0))
-        bb_matmul(of_rows(1, 1))
-        add_w_sum(0, 2)
-        add_w_sum(0, 3)
-        copy_w_sum(1, 0)
-        copy_w_sum(1, 1)
-        w_matmul(1, 2)
-        w_matmul(1, 3)
-        add_bb_sum(1, 0)
-        add_bb_sum(1, 1)
-        copy_bb_sum(of_rows(1, 1)[0:2])
-        copy_bb_sum(of_rows(1, 1)[2:4])
-        add_w_sum(1, 2)
-        add_w_sum(1, 3)
+
+        for pair in range(2):
+            if pair == 0:
+                bb_matmul(0, 0)
+                bb_matmul(0, 1)
+            copy_w_sum(pair, 0)
+            copy_w_sum(pair, 1)
+            w_matmul(pair, 2)
+            w_matmul(pair, 3)
+            if pair == 0:
+                w_matmul(1, 0)
+                w_matmul(1, 1)
+            add_bb_sum(pair, 0)
+            add_bb_sum(pair, 1)
+            copy_bb_sum(pair, 2)
+            copy_bb_sum(pair, 3)
+            if pair == 0:
+                bb_matmul(1, 0)
+                bb_matmul(1, 1)
+            add_w_sum(pair, 2)
+            add_w_sum(pair, 3)

@@ -172,10 +172,10 @@ def tile_rows_lora_bias_kernel(tc, x, w, a, bb, b, out):
                 row_banks_of[(pair, t)] = [bank[:, 2 * (t % 2):2 * (t % 2 + 1), :] for bank in banks]
                 m_cols = slice(P * t, P * (t + 1))
                 m_scale_words = slice(M + P // 4 * t, M + P // 4 * (t + 1))
-                for i in range(2):
-                    c = 2 * pair + i
-                    for half in range(2):
-                        rows = slice(ROWS * half, ROWS * (half + 1))
+                for half in range(2):
+                    rows = slice(ROWS * half, ROWS * (half + 1))
+                    for i in range(2):
+                        c = 2 * pair + i
                         nc.tensor.matmul_mx(out=banks[half][:, 2 * (t % 2) + i, :],
                                             lhsT=bb_packed[rows, m_cols].bitcast(FP8X4),
                                             lhsT_scale=bb_packed[rows, m_scale_words].bitcast(U8),

@@ -115,8 +115,8 @@ def tile_rows_lora_bias_kernel(tc, x, w, a, bb, b, out):
                                   in_=grouped["bb"][:])
 
         def spread_bb():
-            nc.sync.dma_start(out=bb_packed[3 * QUAD:P, :].bitcast(I32), in_=bb_packed[QUAD:2 * QUAD, :].bitcast(I32))
             nc.sync.dma_start(out=bb_packed[0:QUAD, :].bitcast(I32), in_=bb_packed[2 * QUAD:3 * QUAD, :].bitcast(I32))
+            nc.sync.dma_start(out=bb_packed[3 * QUAD:P, :].bitcast(I32), in_=bb_packed[QUAD:2 * QUAD, :].bitcast(I32))
 
         def transpose_bias():
             nc.vector.transpose(out=bias[:], in_=bias_rows[:])
@@ -168,12 +168,14 @@ def tile_rows_lora_bias_kernel(tc, x, w, a, bb, b, out):
 
         def bb_matmul(pair, u):
             banks = row_banks[len(row_banks_of) // 2 % ROW_SETS]
-            for t in (2 * u, 2 * u + 1):
+            tiles = (2 * u, 2 * u + 1)
+            for t in tiles:
                 row_banks_of[(pair, t)] = [bank[:, 2 * (t % 2):2 * (t % 2 + 1), :] for bank in banks]
-                m_cols = slice(P * t, P * (t + 1))
-                m_scale_words = slice(M + P // 4 * t, M + P // 4 * (t + 1))
-                for half in range(2):
-                    rows = slice(ROWS * half, ROWS * (half + 1))
+            for half in range(2):
+                rows = slice(ROWS * half, ROWS * (half + 1))
+                for t in tiles:
+                    m_cols = slice(P * t, P * (t + 1))
+                    m_scale_words = slice(M + P // 4 * t, M + P // 4 * (t + 1))
                     for i in range(2):
                         c = 2 * pair + i
                         nc.tensor.matmul_mx(out=banks[half][:, 2 * (t % 2) + i, :],

@@ -21,6 +21,7 @@ PACK = 4
 GROUP = 256
 COLS = 128
 STRIPS = 2 * PACK + 1
+SHIFT = 32
 WHOLE_BANKS = 4
 ROW_SETS = 2
 
@@ -43,13 +44,14 @@ def tile_rows_lora_bias_kernel(tc, x, w, a, bb, b, out):
         grouped = {name: keep.tile([P, (M if name == "bb" else GROUP) * PACK], BF16, name="grouped_" + name, align_bytes=64)
                    for name in names}
         plain = ("w0", "w1", "x0", "x1", "x2", "x3")
-        codes = {name: keep.tile([P, GROUP], U32, name="codes_" + name, align_bytes=256) for name in plain}
+        codes = {name: keep.tile([P, SHIFT + GROUP], U32, name="codes_" + name, align_bytes=256) for name in plain}
+        codes = {name: tile[:, SHIFT:] if name[0] == "x" else tile[:, 0:GROUP] for name, tile in codes.items()}
         scales = {name: keep.tile([P, GROUP], U8, name="scales_" + name, align_bytes=256) for name in plain}
         a_codes = keep.tile([P, STRIPS * ROWS], U32, name="a_codes", align_bytes=256)
         a_scales = keep.tile([P, STRIPS * ROWS], U8, name="a_scales", align_bytes=256)
         bb_packed = keep.tile([P, M + M // 4], U32, name="bb_packed", align_bytes=256)
         z_grouped = [keep.tile([P, COLS * PACK], BF16, name="z_grouped%d" % c, align_bytes=64) for c in range(4)]
-        z_codes = [keep.tile([P, COLS], U32, name="z_codes%d" % c, align_bytes=256) for c in range(4)]
+        z_codes = [keep.tile([P, SHIFT + COLS], U32, name="z_codes%d" % c, align_bytes=256)[:, SHIFT:] for c in range(4)]
         z_scales = [keep.tile([P, COLS], U8, name="z_scales%d" % c, align_bytes=256) for c in range(4)]
         bias = keep.tile([P, P], F32, name="bias", align_bytes=64)
         bias_rows = keep.tile([P, P], F32, name="bias_rows", align_bytes=64)
@@ -102,7 +104,7 @@ def tile_rows_lora_bias_kernel(tc, x, w, a, bb, b, out):
                 nc.vector.tensor_copy(out=dst[:, 1 - g], in_=src[:, g])
 
         def quantize(name):
-            nc.vector.quantize_mx(out=codes[name][:].bitcast(FP8X4), scales=scales[name][:], in_=grouped[name][:])
+            nc.vector.quantize_mx(out=codes[name].bitcast(FP8X4), scales=scales[name][:], in_=grouped[name][:])
 
         def quantize_a():
             for s in range(PACK):
@@ -152,7 +154,7 @@ def tile_rows_lora_bias_kernel(tc, x, w, a, bb, b, out):
                            in_=whole_bank_of[c].rearrange("p s n -> p n s"))
 
         def z_quantize(c):
-            nc.vector.quantize_mx(out=z_codes[c][:].bitcast(FP8X4), scales=z_scales[c][:], in_=z_grouped[c][:])
+            nc.vector.quantize_mx(out=z_codes[c].bitcast(FP8X4), scales=z_scales[c][:], in_=z_grouped[c][:])
 
         def w_matmul(pair, t):
             bank = next_whole_bank()

@@ -129,13 +129,6 @@ def tile_rows_lora_bias_kernel(tc, x, w, a, bb, b, out):
         def next_whole_bank():
             return whole_banks[len(whole_bank_of) % WHOLE_BANKS]
 
-        def warm_up():
-            bank = next_whole_bank()
-            for s in range(PACK):
-                nc.tensor.matmul_mx(out=bank[:, COLS * s:COLS * (s + 1)], lhsT=a_codes[:, 0:P].bitcast(FP8X4),
-                                    lhsT_scale=a_scales[:, 0:P], rhs=a_codes[:, 0:COLS].bitcast(FP8X4),
-                                    rhs_scale=a_scales[:, 0:COLS], start=True, stop=True)
-
         def z_matmul(c):
             name = "x%d" % c
             bank = next_whole_bank()[:].rearrange("p (s n) -> p s n", s=PACK)
@@ -234,8 +227,6 @@ def tile_rows_lora_bias_kernel(tc, x, w, a, bb, b, out):
         z_matmul(0)
         quantize("x1")
         z_matmul(1)
-        warm_up()
-        warm_up()
 
         interleave(SCALAR, "bb", slice(VECTOR_BB_COLS, M))
         interleave(VECTOR, "bb", slice(0, VECTOR_BB_COLS))

from contextlib import ExitStack

import concourse.mybir as mybir

K, R, M, N = 512, 256, 512, 1024
FLOPS = 2 * N * (K * M + K * R + R * M)

F32 = mybir.dt.float32
BF16 = mybir.dt.bfloat16
U32 = mybir.dt.uint32
I32 = mybir.dt.int32
U8 = mybir.dt.uint8
FP8X4 = mybir.dt.float8_e4m3fn_x4
ADD = mybir.AluOpType.add
IDENTITY = mybir.ActivationFunctionType.Identity

P = 128
ROWS = 64
QUAD = 32
PACK = 4
GROUP = 256
COLS = 128
STRIPS = 2 * PACK + 1
SHIFT = 32
WHOLE_BANKS = 4
ROW_SETS = 2

VECTOR_X_COLS = 128
VECTOR_BB_COLS = 352
VECTOR_W0_COLS = 192

VECTOR, SCALAR = "vector", "scalar"
WHOLE = slice(0, GROUP)


def tile_rows_lora_bias_kernel(tc, x, w, a, bb, b, out):
    nc = tc.nc
    with ExitStack() as ctx:
        keep = ctx.enter_context(tc.tile_pool(name="keep", bufs=1))
        psum = ctx.enter_context(tc.psum_pool(name="psum", bufs=1))

        raw = {}
        names = ("bb", "a", "w0", "w1", "x0", "x1", "x2", "x3")
        grouped = {name: keep.tile([P, (M if name == "bb" else GROUP) * PACK], BF16, name="grouped_" + name, align_bytes=64)
                   for name in names}
        plain = ("w0", "w1", "x0", "x1", "x2", "x3")
        codes = {name: keep.tile([P, SHIFT + GROUP], U32, name="codes_" + name, align_bytes=256) for name in plain}
        codes = {name: tile[:, SHIFT:] if name[0] == "x" else tile[:, 0:GROUP] for name, tile in codes.items()}
        scales = {name: keep.tile([P, GROUP], U8, name="scales_" + name, align_bytes=256) for name in plain}
        a_codes = keep.tile([P, STRIPS * ROWS], U32, name="a_codes", align_bytes=256)
        a_scales = keep.tile([P, STRIPS * ROWS], U8, name="a_scales", align_bytes=256)
        bb_packed = keep.tile([P, M + M // 4], U32, name="bb_packed", align_bytes=256)
        z_grouped = [keep.tile([P, COLS * PACK], BF16, name="z_grouped%d" % c, align_bytes=64) for c in range(4)]
        z_codes = [keep.tile([P, SHIFT + COLS], U32, name="z_codes%d" % c, align_bytes=256)[:, SHIFT:] for c in range(4)]
        z_scales = [keep.tile([P, COLS], U8, name="z_scales%d" % c, align_bytes=256) for c in range(4)]
        bias = keep.tile([P, P], F32, name="bias", align_bytes=64)
        bias_rows = keep.tile([P, P], F32, name="bias_rows", align_bytes=64)

        whole_banks = [psum.tile([P, PACK * COLS], F32, name="whole_bank%d" % i) for i in range(WHOLE_BANKS)]
        row_banks = [[psum.tile([P, PACK, COLS], F32, name="row_bank%d%d" % (half, i)) for half in range(2)]
                     for i in range(ROW_SETS)]
        whole_bank_of = {}
        row_banks_of = {}
        y = [keep.tile([P, 4, 2 * GROUP], F32, name="y%d" % pair, align_bytes=64) for pair in range(2)]

        bb_rows = bb.rearrange("(p j) m -> p j m", j=PACK)
        x_rows = x.rearrange("(p j) n -> p j n", j=PACK)
        w_rows = w.rearrange("(p j) m -> p j m", j=PACK)

        def load(prefix, rows, first, count):
            tile = keep.tile([P, PACK, count * GROUP], F32, name="raw_%s%d" % (prefix, first), align_bytes=64)
            nc.sync.dma_start(out=tile[:], in_=rows[:, :, GROUP * first:GROUP * (first + count)])
            for i in range(count):
                raw["%s%d" % (prefix, first + i)] = tile[:, :, GROUP * i:GROUP * (i + 1)]

        def load_a():
            tile = keep.tile([P, PACK, GROUP], F32, name="raw_a", align_bytes=64)
            nc.sync.dma_start(out=tile[:], in_=a.rearrange("(p j) r -> p j r", j=PACK))
            raw["a"] = tile[:]

        raw_bb = keep.tile([P, PACK, M], F32, name="raw_bb", align_bytes=64)
        raw["bb"] = raw_bb[:]

        def load_bb():
            nc.sync.dma_start(out=raw_bb[QUAD:QUAD + ROWS], in_=bb_rows)

        def load_bias():
            nc.gpsimd.dma_start(out=bias_rows[0:P:QUAD, :].rearrange("q (t j) -> q t j", j=QUAD),
                                in_=b.rearrange("(t q j) o -> q t (j o)", t=4, q=P // QUAD))

        def interleave(engine, name, cols):
            dst = grouped[name][:].rearrange("p (c j) -> p c j", j=PACK)[:, cols]
            src = raw[name].rearrange("p j c -> p c j")[:, cols]
            if engine == VECTOR:
                nc.vector.tensor_copy(out=dst.rearrange("p (c i) j -> p c j i", i=4),
                                      in_=src.rearrange("p (c i) j -> p c j i", i=4))
            else:
                nc.scalar.copy(out=dst, in_=src)

        def interleave_a():
            dst = grouped["a"][:].rearrange("p (s g q j) -> p g q s j", s=PACK, g=2, j=PACK)
            src = raw["a"].rearrange("p j (g q s) -> p g q s j", g=2, s=PACK)
            for g in range(2):
                nc.vector.tensor_copy(out=dst[:, 1 - g], in_=src[:, g])

        def quantize(name):
            nc.vector.quantize_mx(out=codes[name].bitcast(FP8X4), scales=scales[name][:], in_=grouped[name][:])

        def quantize_a():
            for s in range(PACK):
                strip = slice(ROWS * (2 * s + 1), ROWS * (2 * s + 2))
                nc.vector.quantize_mx(out=a_codes[:, strip].bitcast(FP8X4), scales=a_scales[:, strip],
                                      in_=grouped["a"][:, ROWS * PACK * s:ROWS * PACK * (s + 1)])

        def quantize_bb():
            nc.vector.quantize_mx(out=bb_packed[:, 0:M].bitcast(FP8X4), scales=bb_packed[:, M:].bitcast(U8),
                                  in_=grouped["bb"][:])

        def spread_bb():
            nc.sync.dma_start(out=bb_packed[0:QUAD, :].bitcast(I32), in_=bb_packed[2 * QUAD:3 * QUAD, :].bitcast(I32))
            nc.sync.dma_start(out=bb_packed[3 * QUAD:P, :].bitcast(I32), in_=bb_packed[QUAD:2 * QUAD, :].bitcast(I32))

        def transpose_bias():
            nc.vector.transpose(out=bias[:], in_=bias_rows[:])

        def bias_of(t):
            return bias[:, QUAD * t:QUAD * t + 1]

        def next_whole_bank():
            return whole_banks[len(whole_bank_of) % WHOLE_BANKS]

        def z_matmul(c):
            name = "x%d" % c
            bank = next_whole_bank()[:].rearrange("p (s n) -> p s n", s=PACK)
            whole_bank_of[c] = bank
            for s in range(PACK):
                for half in range(2):
                    first = ROWS * (2 * s + 1 - half)
                    window = slice(first, first + P)
                    cols = slice(COLS * half, COLS * (half + 1))
                    nc.tensor.matmul_mx(out=bank[:, s, :], lhsT=a_codes[:, window].bitcast(FP8X4),
                                        lhsT_scale=a_scales[:, window], rhs=codes[name][:, cols].bitcast(FP8X4),
                                        rhs_scale=scales[name][:, cols], start=(half == 0), stop=(half == 1))

        def z_copy(c):
            nc.scalar.copy(out=z_grouped[c][:].rearrange("p (n s) -> p n s", s=PACK),
                           in_=whole_bank_of[c].rearrange("p s n -> p n s"))

        def z_quantize(c):
            nc.vector.quantize_mx(out=z_codes[c].bitcast(FP8X4), scales=z_scales[c][:], in_=z_grouped[c][:])

        def w_matmul(pair, t):
            bank = next_whole_bank()
            whole_bank_of[(pair, t)] = bank
            w_name = "w%d" % (t // 2)
            m_cols = slice(P * (t % 2), P * (t % 2 + 1))
            for i in range(4):
                x_name = "x%d" % (2 * pair + i // 2)
                cols = slice(COLS * (i % 2), COLS * (i % 2 + 1))
                nc.tensor.matmul_mx(out=bank[:, COLS * i:COLS * (i + 1)], lhsT=codes[w_name][:, m_cols].bitcast(FP8X4),
                                    lhsT_scale=scales[w_name][:, m_cols], rhs=codes[x_name][:, cols].bitcast(FP8X4),
                                    rhs_scale=scales[x_name][:, cols], start=True, stop=True)

        def bb_matmul(pair, u):
            banks = row_banks[len(row_banks_of) // 2 % ROW_SETS]
            tiles = (2 * u, 2 * u + 1)
            for t in tiles:
                row_banks_of[(pair, t)] = [bank[:, 2 * (t % 2):2 * (t % 2 + 1), :] for bank in banks]
            for half in range(2):
                rows = slice(ROWS * half, ROWS * (half + 1))
                for t in tiles:
                    m_cols = slice(P * t, P * (t + 1))
                    m_scale_words = slice(M + P // 4 * t, M + P // 4 * (t + 1))
                    for i in range(2):
                        c = 2 * pair + i
                        nc.tensor.matmul_mx(out=banks[half][:, 2 * (t % 2) + i, :],
                                            lhsT=bb_packed[rows, m_cols].bitcast(FP8X4),
                                            lhsT_scale=bb_packed[rows, m_scale_words].bitcast(U8),
                                            rhs=z_codes[c][rows, :].bitcast(FP8X4), rhs_scale=z_scales[c][rows, :],
                                            start=True, stop=True)

        def y_half(pair, t, half):
            return y[pair][:, t:t + 1, :].rearrange("p t (i half n) -> p half (t i) n", i=2, half=2)[:, half]

        def store(pair, t):
            nc.sync.dma_start(out=out[P * t:P * (t + 1), 2 * GROUP * pair:2 * GROUP * (pair + 1)], in_=y[pair][:, t, :])

        def copy_w_sum(pair, t):
            nc.scalar.activation(out=y[pair][:, t, :], in_=whole_bank_of[(pair, t)][:], func=IDENTITY, bias=bias_of(t))

        def add_bb_sum(pair, t):
            for half in range(2):
                part = y_half(pair, t, half)
                nc.vector.tensor_tensor(out=part, in0=row_banks_of[(pair, t)][half], in1=part, op=ADD)
            store(pair, t)

        def copy_bb_sum(pair, t):
            for half in range(2):
                nc.scalar.copy(out=y_half(pair, t, half), in_=row_banks_of[(pair, t)][half])

        def add_w_sum(pair, t):
            nc.vector.scalar_tensor_tensor(out=y[pair][:, t, :], in0=whole_bank_of[(pair, t)][:],
                                           scalar=bias_of(t), in1=y[pair][:, t, :], op0=ADD, op1=ADD)
            store(pair, t)

        ctx.enter_context(tc.manual_schedule())

        load_a()
        load("x", x_rows, 0, 2)
        nc.gpsimd.memset(bias_rows[:], 0.0)
        nc.vector.memset(raw_bb[:], 0.0)
        load_bias()
        load_bb()
        load("x", x_rows, 2, 2)
        load("w", w_rows, 0, 1)
        load("w", w_rows, 1, 1)
        nc.vector.memset(bb_packed[:, M:], 0)
        nc.vector.memset(a_codes[:], 0)
        nc.vector.memset(a_scales[:].bitcast(U32), 0)

        interleave_a()
        quantize_a()
        interleave(VECTOR, "x0", WHOLE)
        interleave(SCALAR, "x1", slice(VECTOR_X_COLS, GROUP))
        interleave(VECTOR, "x1", slice(0, VECTOR_X_COLS))
        quantize("x0")
        z_matmul(0)
        quantize("x1")
        z_matmul(1)

        interleave(SCALAR, "bb", slice(VECTOR_BB_COLS, M))
        interleave(VECTOR, "bb", slice(0, VECTOR_BB_COLS))
        transpose_bias()
        quantize_bb()
        spread_bb()
        z_copy(0)

        interleave(VECTOR, "x2", WHOLE)
        interleave(SCALAR, "x3", slice(VECTOR_X_COLS, GROUP))
        z_copy(1)
        interleave(VECTOR, "x3", slice(0, VECTOR_X_COLS))
        quantize("x2")
        z_matmul(2)
        quantize("x3")
        z_matmul(3)

        interleave(SCALAR, "w0", slice(VECTOR_W0_COLS, GROUP))
        interleave(VECTOR, "w0", slice(0, VECTOR_W0_COLS))
        z_quantize(0)
        z_quantize(1)
        z_copy(2)
        z_copy(3)
        quantize("w0")
        w_matmul(0, 0)
        w_matmul(0, 1)
        interleave(VECTOR, "w1", WHOLE)
        z_quantize(2)
        quantize("w1")
        z_quantize(3)

        for pair in range(2):
            if pair == 0:
                bb_matmul(0, 0)
                bb_matmul(0, 1)
            copy_w_sum(pair, 0)
            copy_w_sum(pair, 1)
            w_matmul(pair, 2)
            w_matmul(pair, 3)
            if pair == 0:
                w_matmul(1, 0)
                w_matmul(1, 1)
            add_bb_sum(pair, 0)
            add_bb_sum(pair, 1)
            copy_bb_sum(pair, 2)
            copy_bb_sum(pair, 3)
            if pair == 0:
                bb_matmul(1, 0)
                bb_matmul(1, 1)
            add_w_sum(pair, 2)
            add_w_sum(pair, 3)
